import numpy as np, ml_dtypes
CORES = [113,118,241,246]
N = 4
BF = ml_dtypes.bfloat16
L, C, S, F, T, RB = 192, 2048, 1280, 768, 6, 40
R16 = np.arange(16)[:, None]
def alphabet(rng, A):
    near = rng.integers(0, 256 - A, (8, 16, 1)) + np.arange(A)
    return np.where(rng.random((8, 16, 1)) < 0.5, near, rng.integers(0, 255, (8, 16, A)))
def values(rng, al, n, skew):
    A = al.shape[-1]; ix = np.minimum((A * rng.random((N, 8, 16, n)) ** skew).astype(np.int64), A - 1)
    return np.take_along_axis(np.broadcast_to(al, (N, 8, 16, A)), ix, 3)
def base(rng, A, skew, sizes):
    al = alphabet(rng, A); m = values(rng, al, F, skew); v = values(rng, al, C, skew)
    share = 0.0625 * rng.choice(np.array(sizes), (N, 8, 1, C))
    pt = np.where(rng.random((N, 8, 16, C)) < share, v, 255)
    return rng.integers(0, C, (N, 8, 16, S)), pt, rng.integers(0, C, (N, 8, C)), rng.integers(0, S, (N, 8, C)), m
def keyed(rng):
    h = C // 2; kr = rng.permutation(16)[:8]; b0 = rng.integers(0, 230, 8)
    pt = np.full((N, 8, 16, C), 255); v = rng.integers(0, 255, (N, 8, 16, C - h)); pt[..., h:] = np.where(rng.random(v.shape) < 0.6, v, 255)
    m = rng.integers(0, 255, (N, 8, 16, F))
    for g in range(8):
        pt[:, g, kr[g], :h] = b0[g] + np.arange(h) % 16
        pt[:, g, kr[g], h:] = np.where(rng.random((N, C - h)) < 0.8, b0[g] + np.arange(h, C) % 20, 255)
        m[:, g, kr[g]] = b0[g] + np.arange(F) % 20
    cl = 16 * rng.integers(0, h // 16, (N, 8, 16, S)) + R16
    return cl, pt, rng.integers(h, C, (N, 8, C)), rng.integers(0, S, (N, 8, C)), m
def message(rng, key):
    return key + 20 * rng.integers(0, F // 20, key.shape)
def edge(rng, lo, hi, shape, share):
    return np.where(rng.random(shape) < share, np.where(rng.random(shape) < 0.5, lo, hi), rng.integers(lo, hi + 1, shape))
def boxes(n, ids):
    return np.where(R16 < n[:, :, None, :], ids, 0)
def pack(cl, pt, bo, gs, m, q, n, p, s, w):
    i4 = lambda a: np.ascontiguousarray(a).astype(np.int32)
    bf = lambda a: np.ascontiguousarray(a.reshape(N, 128, -1)).astype(np.float32).astype(BF)
    return {"cl": i4(cl.reshape(N, 128, S)), "pt": bf(pt), "bo": i4(bo), "gs": i4(gs), "m0": bf(m), "q0": i4(q.reshape(N, 128, L)), "n0": i4(n), "p0": i4(p), "s0": i4(s), "w0": i4(w)}
def setup_inputs(rng):
    cl, pt, bo, gs, m = base(rng, 3, 1, [3, 3, 4, 4, 5, 6, 16])
    n = rng.choice(np.array([0, 1, 1, 2, 2, 3, 4, 6, 10, 15, 16, 16]), (N, 8, L))
    p = np.where(rng.random(n.shape) < 0.7, 0, (rng.random(n.shape) * (n + 1)).astype(np.int64)); p = np.minimum(p, n)
    w = np.where(rng.random(n.shape) < 0.6, 0, rng.integers(0, RB + 16, n.shape))
    return pack(cl, pt, bo, gs, m, boxes(n, rng.integers(0, F, (N, 8, 16, L))), n, p, rng.integers(0, S, n.shape), w)
def setup_inputs_spread(rng):
    cl, pt, bo, gs, m = base(rng, 16, 3, [2, 2, 3, 3, 4, 6, 16])
    cl = (C * rng.random(cl.shape) ** 2).astype(np.int64); bo = (C * rng.random(bo.shape) ** 3).astype(np.int64); gs = (S * rng.random(gs.shape) ** 2).astype(np.int64)
    n = np.minimum((17 * rng.random((N, 8, L)) ** 2).astype(np.int64), 16); p = np.minimum((rng.random(n.shape) * (n + 1)).astype(np.int64), n)
    s = np.minimum((S * rng.random(n.shape) ** 4).astype(np.int64), S - 1); w = rng.integers(0, RB + 16, n.shape)
    ids = (F * rng.random((N, 8, 16, L)) ** 2).astype(np.int64)
    return pack(np.minimum(cl, C - 1), pt, np.minimum(bo, C - 1), np.minimum(gs, S - 1), m, boxes(n, np.minimum(ids, F - 1)), n, p, s, w)
def setup_inputs_ends(rng):
    cl = edge(rng, 0, C - 1, (N, 8, 16, S), 0.7); bo = edge(rng, 0, C - 1, (N, 8, C), 0.7); gs = edge(rng, 0, S - 1, (N, 8, C), 0.7); m = edge(rng, 0, 254, (N, 8, 16, F), 0.9)
    v = rng.choice(np.array([0.3, 0.5, 0.6, 0.7, 0.8]), (N, 8, 1, C)); shape = (N, 8, 16, C)
    pt = np.where(rng.random(shape) < v, 255, np.where(rng.random(shape) < 0.5, 0, 254)); pt = np.where(rng.random(shape) < 0.04, rng.integers(0, 256, shape), pt)
    rr = np.array([0, 7, 15]); e0 = rng.choice(np.array([0, 254]), (8, 3)); e1 = rng.choice(np.array([0, 254]), (8, 3)); e1[:, 0] = 254 - e0[:, 0]
    pt[..., 0] = 255; pt[..., C - 1] = 255
    for g in range(8):
        pt[:, g, rr, 0] = e0[g]; pt[:, g, rr, C - 1] = e1[g]
    m[:, 7, rr, 0] = e0[7]; m[:, 7, rr, F - 1] = e1[7]
    cl[:, 7, :, 0] = C - 1; cl[:, 7, :15, S - 1] = 0; cl[:, 7, 15, S - 1] = C - 1; gs[:, 7, C - 1] = S - 1; bo[:, 7, C - 1] = C - 1
    shape = (N, 8, L)
    n = np.where(rng.random(shape) < 0.8, rng.choice(np.array([0, 16, 16]), shape), rng.choice(np.array([1, 2, 15]), shape))
    p = np.where(rng.random(shape) < 0.8, np.where(rng.random(shape) < 0.7, 0, n), np.maximum(n - 1, 0))
    s = edge(rng, 0, S - 1, shape, 0.7)
    w = np.where(rng.random(shape) < 0.75, np.where(rng.random(shape) < 0.6, 0, RB + 15), rng.choice(np.array([RB - 2, RB - 1, RB - 1, RB]), shape))
    ids = edge(rng, 0, F - 1, (N, 8, 16, L), 0.7)
    a = np.array([0, 1, L // 2, L - 2, L - 1]); b = np.array([2, 3, L - 3])
    for z, st, x in ((a, S - 1, F - 1), (b, 0, 0)):
        s[:, 7, z] = st; n[:, 7, z] = 16; p[:, 7, z] = 15; w[:, 7, z] = RB - 1; ids[:, 7, 15, z] = x
    return pack(cl, pt, bo, gs, m, boxes(n, ids), n, p, s, w)
def setup_inputs_corners(rng):
    cl, pt, bo, gs, m = base(rng, 3, 1, [3, 3, 4, 4, 5, 6, 16])
    n = rng.choice(np.array([0, 1, 15, 16]), (N, 8, L)); p = np.choose(rng.integers(0, 3, n.shape), [0 * n, n, np.maximum(n - 1, 0)])
    w = rng.choice(np.array([0, 1, RB - 17, RB - 16, RB - 1, RB, RB + 15]), n.shape); q = boxes(n, rng.integers(0, F, (N, 8, 16, L)))
    s = np.ascontiguousarray(np.argsort(rng.random((N, 8, S)), axis=-1)[..., :L])
    for a in range(N):
        for g in range(8):
            x = np.take_along_axis(q[a, g], np.minimum(p[a, g], 15)[None, :], 0)[0]; o = rng.permutation(C); ex, ne = o[:L], o[L:2 * L]
            v = m[a, g][:, x]; r = rng.integers(0, 16, L); off = np.where(R16 == r, np.where(v < 254, v + 1, v - 1), v)
            hide = (rng.random((16, L)) < 0.5) & (R16 != r) & (rng.random(L) < 0.5)
            pt[a, g][:, ex] = v; pt[a, g][:, ne] = np.where(hide, 255, off)
            first = np.choose(rng.integers(0, 4, L), [16, 15, 0, 1])
            cl[a, g][:, s[a, g]] = np.where(R16 < first, ne, ex)
    return pack(cl, pt, bo, gs, m, q, n, p, s, w)
def setup_inputs_crowd(rng):
    cl, pt, bo, gs, m = keyed(rng); shape = (N, 8, L); a = np.arange(N)
    key = rng.integers(0, 20, (N, 8, 16, L)); key[:, :6] = 0; key[:, 2:4] = 16
    n = rng.integers(0, 17, shape); n[:, :6] = 16; p = np.zeros(shape, np.int64); w = np.zeros(shape, np.int64)
    s = rng.integers(0, S, shape); s[:, :6] = rng.integers(0, S, (N, 6, 1))
    ids = message(rng, key); same = np.array(ids[:, :6, :1, :1]); ids[:, :6] = same
    one = rng.integers(0, L, (N, 8))
    ids[a, 1, :, one[:, 1]] = 19; ids[a, 3, :, one[:, 3]] = 0
    w[:, 4] = RB; w[a, 4, one[:, 4]] = RB - 1
    p[::2, 5] = 16; p[a[::2], 5, one[::2, 5]] = 15; n[a[::2], 5, one[::2, 5]] = 15
    s[:, 6] = rng.choice(np.array([0, S - 1]), (N, L)); ids[:, 6] = rng.choice(np.array([0, 20 * (F // 20) - 20]), (N, 16, L)); gs[:, 6] = rng.choice(np.array([0, S - 1]), (N, C))
    cl[:, 6, :, 0] = 16 * rng.integers(0, C // 32, (N, 1)); cl[:, 6, :, S - 1] = 16 * rng.integers(0, C // 32, (N, 1)); cl[:, 6, 0, S - 1] += 1
    z = (rng.integers(0, N) + np.arange(2)) % N; y = np.array([0, 1, 2, 3, 4, 5, 7])
    n[z] = rng.integers(1, 17, (2, 8, L)); p[z] = 0; w[z] = 0
    ids[z[:, None], y, 0] = message(rng, rng.integers(0, 16, (2, 7, L)))
    for r in range(N):
        if r not in z: pt[r, 7, :, C // 2::4] = 0
    return pack(cl, pt, bo, gs, m, boxes(n, ids), n, p, s, w)
def setup_inputs_calm(rng):
    cl, pt, bo, gs, m = keyed(rng); shape = (N, 8, L); i = np.arange(L)
    e = ((np.arange(8) + np.arange(N)[:, None]) % 4)[:, :, None] + 0 * i
    ty = (i + rng.integers(0, 8, (N, 8, 1))) % 8; j = T - 2 - e % 2
    fj = np.where(R16 < j[:, :, None], 0, 16)
    key = np.choose(ty[:, :, None], [0, fj, fj, 0, 16, 16, 0, rng.integers(0, 20, (N, 8, 16, L))])
    n = np.choose(ty, [16, 16, 16, 16, e + 1, 16, e, rng.integers(14, 17, shape)])
    p = np.choose(ty, [0, 0, 0, 0, 0, 10 + e, 0, np.minimum((rng.random(shape) * (n + 1)).astype(np.int64), n)])
    w = np.choose(ty, [RB - (T - 1 - e), RB - 1 - j, RB - 2 - j, RB - T + e % 2, 0, 0, e, rng.integers(0, RB + 16, shape)])
    return pack(cl, pt, bo, gs, m, boxes(n, message(rng, key)), n, p, rng.integers(0, S, shape), w)
def check_inputs(d):
    bad = []
    for k, lo, hi in (("cl", 0, C - 1), ("pt", 0, 255), ("bo", 0, C - 1), ("gs", 0, S - 1), ("m0", 0, 254), ("q0", 0, F - 1), ("n0", 0, 16), ("p0", 0, 16), ("s0", 0, S - 1), ("w0", 0, RB + 15)):
        v = np.asarray(d[k]).astype(np.float64)
        if not np.all((v >= lo) & (v <= hi)): bad.append("range of " + k)
    for k in ("pt", "m0"):
        v = np.asarray(d[k]).astype(np.float64)
        if np.any(v != np.floor(v)): bad.append("whole numbers of " + k)
    if np.any(d["p0"] > d["n0"]): bad.append("p0 at most n0")
    n = d["n0"].astype(np.int64)[:, :, None, :]; q = d["q0"].astype(np.int64).reshape(N, 8, 16, L)
    if np.any(np.where(R16 >= n, q, 0) != 0): bad.append("0 in empty places of q0")
    return bad
def reference(cl, pt, bo, gs, m0, q0, n0, p0, s0, w0):
    lists_ = cl.astype(np.int64).reshape(N, 8, 16, S); tp = pt.astype(np.float32).astype(np.int64).reshape(N, 8, 16, C)
    M = np.zeros((N, 8, 16, F + T * L), np.int64); M[..., :F] = m0.astype(np.float32).astype(np.int64).reshape(N, 8, 16, F)
    q = q0.astype(np.int64).reshape(N, 8, 16, L); n = n0.astype(np.int64); p = p0.astype(np.int64); s = s0.astype(np.int64); w = w0.astype(np.int64)
    body = bo.astype(np.int64); nxt = gs.astype(np.int64)
    for t in range(T):
        rest = w >= RB; act = ~rest & (p < n)
        x = np.take_along_axis(q, np.minimum(p, 15)[:, :, None, :], 2)
        m = np.take_along_axis(M, x, 3)
        c = np.take_along_axis(lists_, s[:, :, None, :], 3)
        ok = np.ones((N, 8, 16, L), bool)
        for row in range(16):
            g = np.take_along_axis(tp[:, :, row], c.reshape(N, 8, 16 * L), 2).reshape(N, 8, 16, L)
            ok &= (g == 255) | (g == m[:, :, row][:, :, None, :])
        found = act & np.any(ok, axis=2); fail = act & ~found; k = np.argmax(ok, axis=2)
        c1 = np.take_along_axis(c, k[:, :, None, :], 2)[:, :, 0]
        b = np.take_along_axis(tp, np.take_along_axis(body, c1, 2)[:, :, None, :], 3)
        out = np.where(found[:, :, None, :], np.where(b == 255, m, b), 0)
        w = np.where(rest, 0, np.where(found, w + k + 1, np.where(fail, w + 16, w)))
        s = np.where(found, np.take_along_axis(nxt, c1, 2), s)
        up = np.concatenate([q[:, :, 1:], np.zeros((N, 8, 1, L), np.int64)], axis=2)
        q = np.where(found[:, :, None, :] & (R16 >= p[:, :, None, :]), up, q)
        n = n - found; p = np.where(found, 0, np.where(fail, p + 1, p))
        d = 1 + t % (N - 1)
        M[..., F + L * t:F + L * (t + 1)] = np.roll(out, d, axis=0)
        keep = np.roll(found, d, axis=0) & (n < 16)
        q = np.where(keep[:, :, None, :] & (R16 == n[:, :, None, :]), F + L * t + np.arange(L), q)
        n = n + keep
    return {"mn": np.ascontiguousarray(M[..., F:]).reshape(N, 128, T * L).astype(np.float32).astype(BF), "yq": q.reshape(N, 128, L).astype(np.float32),
            "ys": np.concatenate([s, p, n, w], axis=2).astype(np.float32)}

@@ -1,0 +1,532 @@
+import numpy as np
+from concourse.mybir import AluOpType as A, ActivationFunctionType as F
+
+NB = 3
+L = 192 // NB
+W = L // 16
+R = 4
+GC = 2
+KEEP = (1, 3)
+H16 = "float16"
+NS = 6
+BIG = float(2 ** 40)
+ON_S = {"cs": True, "fi": True, "pf": True}
+WN = ["BLK", "I0", "I40", "LE", "TRI", "WPP", "WNN", "WDT", "WDN", "WFP", "WFN", "N4K", "WZS", "WZP2",
+      "WZN2", "WL", "WLX", "WW", "NBL", "RR", "WZZ", "WZF", "WZC", "WZP", "WZN", "WZM"]
+
+SCRATCH = {
+    "ptb": ("sbuf", [128, 2048], "bfloat16"), "fl": ("sbuf", [128, 2048], "bfloat16"), "gt": ("sbuf", [128, 2048], "bfloat16"),
+    "clb": ("sbuf", [128, 1280], "int32"), "xb": ("sbuf", [128, 256], "int32"), "xf": ("sbuf", [128, 256], "float32"),
+    "bw": ("sbuf", [128, 256], "uint16"), "pb": ("sbuf", [128, 2064], "bfloat16"), "zt": ("sbuf", [128, 2064], "bfloat16"),
+    "tc": ("sbuf", [128, 2056], "float32"), "gst": ("sbuf", [128, 2056], "int32"),
+    "ai": ("sbuf", [128, 768], "int32"), "af": ("sbuf", [128, 768], H16), "qi": ("sbuf", [128, 192], "int32"),
+    "qa": ("sbuf", [128, 192], "float32"), "top": ("sbuf", [128, 192], "float32"), "jr": ("sbuf", [128, 192], "float32"),
+    "jb": ("sbuf", [128, 128], "float32"), "jf": ("sbuf", [128, 144], "float32"),
+    "i32": ("sbuf", [128, 128], "float32"), "ic": ("sbuf", [128, 8], "int32"),
+    "fc": ("sbuf", [128, 32], "float32"), "oh": ("sbuf", [128, 16], "float32"),
+    "b1": ("sbuf", [128, 144], "bfloat16"), "b2": ("sbuf", [128, 144], "bfloat16"),
+    "wt": ("sbuf", [128, 128 * len(WN)], "bfloat16"),
+    "mc": ("sbuf", [128, 192], "bfloat16"), "mx": ("sbuf", [128, 192], H16), "rs": ("sbuf", [128, 192], "float32"),
+    "tf": ("sbuf", [128, 192], H16), "dg": ("sbuf", [128, 192], "float32"), "e0": ("sbuf", [128, 192], H16),
+    "outb": ("sbuf", [128, 2304], "bfloat16"),
+    "yqb": ("sbuf", [128, 192], "float32"), "ysb": ("sbuf", [128, 768], "float32"),
+}
+for _b in range(NB):
+    for _n, _s, _d in (("mm", [128, 1920], "bfloat16"), ("gg", [128, 16 * L], "bfloat16"), ("ee", [128, 16 * L], "bfloat16"),
+                       ("cf", [128, L], H16), ("cu", [128, L], "uint16"), ("xx", [128, L], "float32"),
+                       ("ok", [128, L], "bfloat16"), ("cs", [128, L], H16),
+                       ("sc", [128, L], "float32"), ("sx", [128, L], "float32"), ("ix", [128, 16], "uint16"),
+                       ("iy", [128, 16], "uint16"), ("mv", [128, L], "bfloat16"), ("bt", [128, L], "bfloat16"),
+                       ("pf", [128, 14 * L], "bfloat16"), ("t1", [128, 6 * L], H16), ("pd", [128, L], H16), ("dq", [128, L], H16),
+                       ("zz", [128, L], H16), ("zp", [128, L], H16), ("f2", [128, L], "bfloat16")):
+        SCRATCH[_n + str(_b)] = ("sbuf", _s, _d)
+for _b in range(8):
+    SCRATCH["ps" + str(_b)] = ("psum", [128, 512], "float32")
+
+SEMAPHORES = (["cV", "cS", "cP", "cG", "sent"] + ["d%d" % _i for _i in range(60)]
+              + ["a%d_%d" % (_b, _t) for _b in range(NB) for _t in range(NS)])
+
+COST = {"cy": 1.0, "v0": 25.0, "s0": 70.0, "g": 1.56, "pe": 0.5, "hop": 140.0, "self": 85.0, "rem": 2600.0, "rem0": 2500.0,
+        "dma": 1900.0, "bw": 230.0, "skews": [1500.0, 2400.0, 3300.0], "rounds": 100, "noise": 150.0, "seed": 1}
+
+
+def place(name, b):
+    if NB == 2:
+        bank, reg = {"m": (0, 0), "sc": (1, 0), "fi": (1, 1), "cr": (1, 2), "xr": (1, 3), "yn": (1, 4), "fd": (2, 0),
+                     "P": (2, 2), "F": (2, 3), "u": (2, 4), "z": (2, 4), "dq": (6 + b, 0)}[name]
+        return (bank, reg) if bank > 5 else (3 * b + bank, reg)
+    bank, reg = {"m": (0, 0), "fd": (0, 4), "P": (0, 6), "F": (0, 7), "sc": (1, 0), "fi": (1, 1), "cr": (1, 2),
+                 "xr": (1, 3), "yn": (1, 4), "u": (1, 5), "z": (6 + b % 2, b), "dq": (1, 6)}[name]
+    return (bank, reg) if bank > 5 else (2 * b + bank, reg)
+
+
+def build(g, T, send):
+    ops, wr, rd, bank, cur = [], {}, {}, {}, [0]
+    cy = COST["cy"]
+
+    def add(eng, fn, reads, writes, cost, banks=(), lat=0.0, sem=None):
+        i = len(ops)
+        dep, order = set(), set()
+        for t in reads:
+            if t in wr: dep.add(wr[t])
+        for t in writes:
+            if t in wr: dep.add(wr[t])
+            dep.update(rd.get(t, ()))
+        for b in banks:
+            last = bank.setdefault(b, {})
+            for e, j in last.items():
+                if e != eng: dep.add(j)
+                else: order.add(j)
+            last[eng] = i
+        for t in reads: rd.setdefault(t, []).append(i)
+        for t in writes:
+            wr[t] = i; rd[t] = []
+        dep.discard(i)
+        ops.append({"e": eng, "fn": fn, "dep": dep, "ord": order, "c": cost, "lat": lat, "sem": sem, "b": cur[0], "w": writes})
+        return i
+
+    def n_of(ap):
+        n = 1
+        for s in ap.shape[1:]: n *= s
+        return n
+
+    def vcost(n, f): return COST["v0"] + max(64.0, n * f) * cy
+
+    def ts(out, in0, s1, s2, op0, op1, r, w, f=1.0, banks=(), gather=False):
+        if op1 is None: fn = lambda: g.vector.tensor_scalar(out, in0, s1, None, op0)
+        else: fn = lambda: g.vector.tensor_scalar(out, in0, s1, s2, op0, op1)
+        add("V", fn, r, w, 50.0 + n_of(out) * COST["g"] * cy if gather else vcost(n_of(out), f), banks)
+
+    def tt(out, in0, in1, op, r, w, banks=(), gather=False):
+        n = n_of(out)
+        c = 50.0 + n * COST["g"] * cy if gather else vcost(n, 1.0 if banks else 2.0)
+        add("V", lambda: g.vector.tensor_tensor(out, in0, in1, op), r, w, c, banks)
+
+    def cp(out, in_, r, w, f=1.0, banks=(), gather=False):
+        n = n_of(out)
+        add("V", lambda: g.vector.tensor_copy(out, in_), r, w, 50.0 + n * COST["g"] * cy if gather else vcost(n, f), banks)
+
+    def act(out, in_, func, r, w, bias=0.0, scale=1.0, banks=(), gather=False, extra=0.0):
+        c = COST["s0"] + n_of(out) * cy * (COST["g"] if gather else 1.0) + extra
+        add("S", lambda: g.scalar.activation(out, in_, func, bias=bias, scale=scale), r, w, c, banks)
+
+    def mm(b, out, terms, first=True, last=True):
+        for j, (lh, rh, r, k) in enumerate(terms):
+            st, sp = first and j == 0, last and j == len(terms) - 1
+            add("P", lambda lh=lh, rh=rh, st=st, sp=sp: g.tensor.matmul(out, lh, rh, st, sp), r, [],
+                max(64.0, n_of(rh)) * COST["pe"] * k, [b])
+
+    def iota(out, pat, base, mul, w, fl=True):
+        if fl: fn = lambda: g.iota(out, pat, base, mul, allow_small_or_imprecise_dtypes=True)
+        else: fn = lambda: g.iota(out, pat, base, mul)
+        add("G", fn, [], w, 130.0 + 2 * n_of(out) * cy)
+
+    def fill(out, v, w, fl=True): iota(out, [[0, n_of(out)]], v, 0, w, fl)
+
+    def band(n, src, sign, base, op, other):
+        add("G", lambda: g.affine_select(Wt(n), Wt(src), [[sign, 128]], op, other, base, -sign), [src], [n], 170.0 + 256 * cy)
+
+    nd, queued = [0], [0.0]
+
+    def dma(q, out, in_, r, w, nbytes, load=True):
+        s = "d%d" % nd[0]; nd[0] += 1
+        eng = g.sync if q == "Y" else g.scalar
+        if load: queued[0] += nbytes / COST["bw"]
+        lat = COST["dma"] + (queued[0] if load else nbytes / COST["bw"])
+        add(q, lambda: eng.dma_start(out, in_), r, w, 60.0, lat=lat, sem=(s, 16), banks=["q" + q] if load else [])
+
+    def Wt(n, rows=128):
+        j = WN.index(n)
+        return T.wt[0:rows, 128 * j:128 * j + 128]
+
+    def Wc(n, r):
+        j = WN.index(n)
+        return T.wt[:, 128 * j + r:128 * j + 128:16]
+
+    def ps(name, b, n=1):
+        k, a = place(name, b)
+        return T["ps%d" % k][:, a * L:(a + n) * L]
+
+    bk = lambda name, b: place(name, b)[0]
+    DQ = lambda b: ps("dq", b)
+
+    def pm(name, b, terms, first=True, last=True): mm(bk(name, b), ps(name, b), terms, first, last)
+
+    for j, n in enumerate(("s0", "p0", "n0", "w0")):
+        dma("S", T.ai[0:8, 192 * j:192 * j + 192], T[n][:], [], ["ai%d" % j], 6144)
+    for k in range(8):
+        dma("S", T.xb[:, 16 * k:16 * k + 16], T.bo[k, :], [], ["xb%d" % k], 16384)
+    for h in range(2):
+        dma("Y", T.ptb[:, 1024 * h:1024 * h + 1024], T.pt[:, 1024 * h:1024 * h + 1024], [], ["pt%d" % h], 262144)
+    dma("S", T.qi[:], T.q0[:], [], ["qi"], 98304)
+    for k in range(8):
+        dma("Y", T.xb[:, 128 + 16 * k:144 + 16 * k], T.gs[k, :], [], ["xb%d" % (8 + k)], 16384)
+    dma("Y", T.clb[:], T.cl[:], [], ["cl"], 655360)
+    dma("Y", T.mm0[:, 0:768], T.m0[:], [], ["m0_0"], 196608)
+    for b in range(1, NB):
+        dma("Y", T["mm%d" % b][:, 0:768], T.m0[:], [], ["m0_%d" % b], 196608)
+
+    names = ["g16", "x", "p16", "f1", "f2", "f5", "c1", "c2", "hi", "f23", "f40", "fp", "xm", "xn", "u0", "u1", "u2", "u3", "u4",
+             "k0", "k1", "k2", "k3", "k4", "k5"]
+    fc = lambda n: T.fc[:, names.index(n):names.index(n) + 1]
+    oh = lambda k: T.oh[:, k:k + 1]
+    iota(T.ic[:, 0:1], [[1, 1]], 0, 1, ["p"], False)
+    iota(T.jb[:], [[16, 8], [0, 16]], 0, 0, ["jb"])
+    iota(T.jr[:], [[0, 12], [1, 16]], 0, 0, ["jr"])
+    iota(T.rs[:, 0:L], [[0, W], [4096, 16]], 0, 0, ["rs"])
+    iota(T.jf[:], [[1, 144]], -15, 0, ["jf"])
+    iota(T.top[:], [[1, 192]], 576, 0, ["top"])
+    iota(T.dg[:], [[1, 192]], 1600, 0, ["dg"])
+    iota(fc("p16"), [[1, 1]], 0, 16, ["p16"])
+    for c in range(4): fill(T.gst[:, 514 * c:514 * c + 514], -1, ["gs%d" % c], False)
+    dma("Y", T.gst[0:128:16, 0:2048], T.gs[:], [], ["gs%d" % c for c in range(4)], 65536, False)
+    ts(T.ic[:, 1:2], T.ic[:, 0:1], 112, None, A.bitwise_and, None, ["p"], ["ic1"])
+    ts(T.ic[:, 2:3], T.ic[:, 0:1], 15, None, A.bitwise_and, None, ["p"], ["ic2"])
+    cp(T.fc[:, 0:2], T.ic[:, 1:3], ["ic1", "ic2"], ["g16", "x"])
+    ts(Wt("BLK"), T.jb[:], fc("g16"), None, A.is_equal, None, ["jb", "g16"], ["BLK"])
+    ts(Wt("RR", 8), T.jb[0:8, :], T.fc[0:8, 2:3], None, A.is_equal, None, ["jb", "p16"], ["RR"])
+    ts(T.b1[:], T.jf[:], fc("g16"), None, A.is_equal, None, ["jf", "g16"], ["b1"])
+    act(T.b2[:], T.b1[:], F.Identity, ["b1"], ["b2"], scale=1.0 / BIG)
+    band("I0", "BLK", 1, 0, A.is_equal, 0.0)
+    act(Wt("I40"), Wt("I0"), F.Identity, ["I0"], ["I40"], scale=BIG)
+    act(T.i32[:], Wt("I0"), F.Identity, ["I0"], ["i32"], scale=-1.0)
+    act(Wt("N4K"), Wt("I0"), F.Identity, ["I0"], ["N4K"], scale=-4096.0)
+    act(Wt("NBL"), Wt("BLK"), F.Identity, ["BLK"], ["NBL"], scale=-1.0)
+    band("WDT", "BLK", 1, 1, A.is_equal, 0.0); band("WDT", "WDT", 1, 0, A.not_equal, -1.0)
+    band("TRI", "NBL", 1, 0, A.is_gt, 0.0); band("TRI", "TRI", 1, 0, A.not_equal, 1.0)
+    band("WPP", "BLK", 1, 0, A.is_ge, 0.0); band("WPP", "WPP", -1, 1, A.is_ge, 0.0)
+    band("WNN", "BLK", 1, 1, A.is_ge, 0.0); band("WNN", "WNN", -1, 1, A.is_ge, 0.0)
+    band("LE", "BLK", -1, 0, A.is_ge, 0.0)
+    act(Wt("WDN"), Wt("WDT"), F.Identity, ["WDT"], ["WDN"], scale=192.0)
+    act(Wt("WFP"), Wt("BLK"), F.Identity, ["BLK"], ["WFP"], scale=3.0)
+    act(Wt("WFN"), Wt("BLK"), F.Identity, ["BLK"], ["WFN"], scale=-1.0)
+    act(Wc("WFN", 15), Wc("BLK", 0), F.Identity, ["BLK"], ["WFN"], scale=-2.0)
+    ts(T.oh[:], T.jr[:, 0:16], fc("x"), None, A.is_equal, None, ["jr", "x"], ["oh"])
+
+    def col(n, k, c, prev):
+        act(fc(n), oh(k), F.Identity, ["oh"] + ([prev] if isinstance(prev, str) else []), [n], scale=c,
+            bias=oh(prev) if isinstance(prev, int) else fc(prev))
+    col("u0", 3, 16.0, 1); col("u1", 2, 128.0, "u0"); col("f1", 0, -128.0, "u1")
+    ts(fc("f2"), oh(0), 40.0, fc("f1"), A.mult, A.subtract, ["oh", "f1"], ["f2"])
+    col("f5", 5, 1.0, 6); col("c1", 2, -1.0, 1); col("u2", 2, 40.0, 0); col("c2", 3, -17.0, "u2")
+    col("u3", 1, 1.0, "f5"); ts(fc("hi"), fc("u3"), 4095.0, 1.0, A.mult, A.add, ["u3"], ["hi"])
+    col("f23", 2, 1.0, 3); col("f40", 0, -1.0, 4)
+    ts(fc("fp"), oh(15), 1.0, None, A.add, None, ["oh"], ["fp"])
+    act(fc("u4"), oh(0), F.Identity, ["oh"], ["u4"], scale=-17.0)
+    ts(fc("xm"), fc("x"), -15.0, None, A.add, None, ["x"], ["xm"])
+    act(fc("xn"), fc("xm"), F.Identity, ["xm"], ["xn"], scale=-1.0)
+    ts(fc("k4"), fc("x"), 512.0, 256.0, A.mult, A.add, ["x"], ["k4"])
+    ts(fc("k5"), fc("x"), -512.0, -256.0, A.mult, A.add, ["x"], ["k5"])
+    for n in ("WZP", "WZN", "WZZ", "WZF", "WZC", "WZM"): fill(Wt(n), 0, ["z" + n])
+
+    def wcol(n, r, c):
+        s, tk = (c, []) if isinstance(c, float) else ((oh(c), ["oh"]) if isinstance(c, int) else (fc(c), [c]))
+        act(Wc(n, r), Wc("BLK", 0), F.Identity, ["BLK", "z" + n] + tk, [n + str(r)], scale=s)
+    zc = [("WZZ", 0, 0), ("WZZ", 1, "f1"), ("WZZ", 2, "f2"), ("WZZ", 3, "u4"), ("WZZ", 5, "f5"),
+          ("WZF", 1, "xm"), ("WZF", 2, "xn"), ("WZF", 5, -4096.0), ("WZC", 6, 1.0), ("WZP", 3, "fp"), ("WZN", 3, 1.0),
+          ("WZM", 3, 1.0), ("WZM", 4, 1.0)]
+    for n, r, c in zc: wcol(n, r, c)
+    zt_ = lambda n: [a + str(r) for a, r, c in zc if a == n]
+    act(Wt("WZS"), Wt("BLK"), F.Identity, ["BLK", "f23"], ["WZS"], scale=fc("f23"))
+    act(Wt("WZP2"), Wt("WZS"), F.Identity, ["WZS"], ["WZP2"], scale=-0.5)
+    act(Wt("WZN2"), Wt("BLK"), F.Identity, ["BLK", "f40"], ["WZN2"], scale=fc("f40"))
+    act(Wc("WZN2", 0), Wc("BLK", 0), F.Identity, ["BLK", "oh"], ["WZN2"], scale=oh(4))
+    act(Wt("WL"), Wt("BLK"), F.Identity, ["BLK", "f5"], ["WL"], scale=fc("f5"))
+    act(Wt("WLX"), Wt("WL"), F.Identity, ["WL"], ["WLX"], scale=-2048.0)
+    act(Wt("WW"), Wt("BLK"), F.Identity, ["BLK", "oh"], ["WW"], scale=oh(1))
+    ts(T.mc[:], T.jr[:], fc("x"), -8192.0, A.not_equal, A.mult, ["jr", "x"], ["mc"])
+    tt(T.mx[:], T.dg[:], T.mc[:], A.add, ["dg", "mc"], ["mx"])
+    ts(T.tf[:], T.top[:], 1152.0, None, A.add, None, ["top"], ["tf"])
+    fill(T.pb[:, 2048:2064], 0, ["pbx"]); fill(T.tc[:, 2048:2056], -1, ["tcx"]); fill(T.zt[:, 2048:2064], 0, ["ztx"])
+    fill(fc("k0"), -128, ["k0"]); fill(fc("k1"), -17 * 4096, ["k1"]); fill(fc("k2"), -2048, ["k2"]); fill(fc("k3"), 16, ["k3"])
+    lo = lambda b: L * b if b < NB - 1 else L * b - L
+    fills = [[[] for _ in range(NS)] for _ in range(NB)]
+    for b in range(NB):
+        edges = [768]
+        for t in range(NS - 1): edges += [768 + 192 * t + lo(b), 768 + 192 * t + lo(b) + 2 * L]
+        for j in range(0, len(edges) - 1, 2):
+            if edges[j + 1] > edges[j]:
+                for t in range(j // 2 + 1, NS): fills[b][t].append("mz%d_%d" % (b, j))
+                fill(T["mm%d" % b][:, edges[j]:edges[j + 1]], 0, ["mz%d_%d" % (b, j)])
+
+    tb = [7, 6, 7, 6]
+    for c in range(4):
+        sl = slice(512 * c, 512 * c + 512); tk = "pt%d" % (c // 2)
+        ts(T.fl[:, sl], T.ptb[:, sl], 255.0, None, A.is_equal, None, [tk], ["fl%d" % c], 0.5)
+        mm(tb[c], T["ps%d" % tb[c]][:], [(Wt("I0"), T.ptb[:, sl], ["I0", tk], 1), (Wt("I40"), T.fl[:, sl], ["I40", "fl%d" % c], 1)])
+        if c % 2: cp(T.gt[:, sl], T["ps%d" % tb[c]][:], [], ["gt%d" % c], banks=[tb[c]])
+        else: act(T.gt[:, sl], T["ps%d" % tb[c]][:], F.Identity, [], ["gt%d" % c], banks=[tb[c]])
+    GT = ["gt%d" % c for c in range(4)]
+    cp(T.af[0:8, 0:192], T.ai[0:8, 0:192], ["ai0"], ["af0"])
+    cp(T.af[0:8, 192:768], T.ai[0:8, 192:768], ["ai1", "ai2", "ai3"], ["af1"])
+    tt(T.qa[:], T.top[:], T.qi[:], A.subtract, ["top", "qi"], ["qa"])
+    for h in range(2):
+        sl = slice(128 * h, 128 * h + 128); kb = bk("sc", NB - 1); pb_ = T["ps%d" % kb][:, 128 * h:128 + 128 * h]
+        cp(T.xf[:, sl], T.xb[:, sl], ["xb%d" % (8 * h + k) for k in range(8)], ["xf%d" % h])
+        mm(kb, pb_, [(T.xf[:, sl], T.i32[:], ["xf%d" % h, "i32"], 4)])
+        ts(T.bw[:, sl], pb_, -1.0, None, A.mult, None, [], ["bw%d" % h], banks=[kb])
+    for c in range(4):
+        sl = slice(512 * c, 512 * c + 512)
+        act(T.pb[:, sl], T.ptb[:].indirect(T.bw[:, 32 * c:32 * c + 32]), F.Identity, ["pt0", "pt1", "bw0"], ["pb%d" % c], gather=True)
+        ts(T.zt[:, sl], T.pb[:, sl], 255.0, 256.0, A.not_equal, A.mult, ["pb%d" % c], ["zt%d" % c], 0.5)
+        ts(T.tc[:, sl], T.clb[:].indirect(T.bw[:, 128 + 32 * c:160 + 32 * c]), 1.0 / 4096, None, A.mult, None, ["cl", "bw1"], ["tc%d" % c], gather=True)
+    PB = ["pb%d" % c for c in range(4)] + ["pbx"]
+    ZT = ["zt%d" % c for c in range(4)] + ["ztx"]
+    TC = ["tc%d" % c for c in range(4)] + ["tcx"]
+
+    def wrap(b, reg, buf, idx, s1, s2, op0, op1):
+        sb = str(b); o = T[buf + sb]
+        add("V", lambda: g.vector.tensor_tensor_scan(o[:], T.rs[:, 0:L], ps(reg, b), 0.0, A.min, A.max),
+            ["rs"], [buf + sb], vcost(L, 1.0), [bk(reg, b)])
+        ts(T[idx + sb][:, 0:W], o[:, 15:L:16], s1, s2, op0, op1, [buf + sb], [idx + sb])
+
+    past = [[(Wt("WDT"), T.e0[:, L * b:L * b + L], ["WDT", "e0%d" % b], 1)] for b in range(NB)]
+
+    def look(b, s):
+        sb = str(b); c0 = L * b
+        tt(T["pd" + sb][:], T["pf" + sb][:, 2 * L * s:2 * L * s + L], DQ(b), A.mult, ["P%s_%d" % (sb, s)], ["pd" + sb], [bk("dq", b)])
+        if s - 1 in KEEP:
+            act(T["dq" + sb][:], DQ(b), F.Identity, [], ["dq" + sb], banks=[bk("dq", b)])
+            past[b][:] = [(Wt("I0"), T["dq" + sb][:], ["I0", "dq" + sb], 1)]
+        pm("xr", b, [(Wt("I0"), T.mx[:, c0:c0 + L], ["I0", "mx"], 1), (Wt("BLK"), T["pd" + sb][:], ["BLK", "pd" + sb], 1)])
+        wrap(b, "xr", "sx", "iy", 192.0 * s - 1024.0, None, A.add, None)
+
+    def zlayer(b, out, terms):
+        pm("z", b, terms)
+        ts(T[out + str(b)][:], ps("z", b), 0.0, fc("hi"), A.max, A.min, ["hi"], [out + str(b)], banks=[bk("z", b)])
+
+    once = [1300.0]
+
+    def step01(out, name, b, n, w):
+        if ON_S["pf"]:
+            act(out, ps(name, b, n), F.Sigmoid, ["k0"], w, bias=fc("k0"), scale=512.0, banks=[bk(name, b)], extra=once[0]); once[0] = 0.0
+        else: ts(out, ps(name, b, n), 0.5, None, A.is_ge, None, [], w, banks=[bk(name, b)])
+
+    for b in range(NB):
+        sb = str(b); c0 = L * b; cur[0] = b
+        a_ = lambda j: T.af[0:8, 192 * j + c0:192 * j + c0 + L]
+        pm("cr", b, [(Wt("I0"), T.mc[:, 0:L], ["I0", "mc"], 1), (Wt("RR", 8), a_(0), ["RR", "af0"], 1)])
+        wrap(b, "cr", "sc", "ix", 0.0, None, A.add, None)
+        cp(T["cu" + sb][:], T.clb[:].indirect(T["ix" + sb][:, 0:W]), ["cl", "ix" + sb], ["cu" + sb], gather=True)
+        ts(T["cf" + sb][:], T["cu" + sb][:], 1.0 / 4096, None, A.mult, None, ["cu" + sb], ["cf" + sb], 0.5)
+        for j, nm in enumerate(("P", "F", "fd")): pm(nm, b, [(Wt("RR", 8), a_(1 + j), ["RR", "af1"], 1)])
+        act(T["pf" + sb][:, 0:L], ps("P", b), F.Sigmoid, ["k4"], ["P%s_0" % sb], bias=fc("k4"), scale=-512.0, banks=[bk("P", b)], extra=once[0])
+        once[0] = 0.0
+        act(T["pf" + sb][:, L:2 * L], ps("F", b), F.Sigmoid, ["k5"], ["F%s_0" % sb], bias=fc("k5"), scale=512.0, banks=[bk("F", b)])
+        ts(T["zp" + sb][:], ps("fd", b), fc("c1"), fc("c2"), A.mult, A.add, ["c1", "c2"], ["zp" + sb], banks=[bk("fd", b)])
+        tt(T.e0[:, c0:c0 + L], T.qa[:, c0:c0 + L], T["pf" + sb][:, L:2 * L], A.mult, ["qa", "F%s_0" % sb], ["e0" + sb])
+        pm("dq", b, past[b])
+        look(b, 0)
+        zlayer(b, "zz", [(Wt("I0"), T["zp" + sb][:], ["I0", "zp" + sb], 1), (Wt("WZP"), T["pf" + sb][:, 0:L], zt_("WZP") + ["P%s_0" % sb], 1),
+                         (Wt("WZN"), T["pf" + sb][:, L:2 * L], zt_("WZN") + ["F%s_0" % sb], 1)])
+
+    LC = L // GC
+    KS = 16 // R
+    for t in range(NS):
+        for b in range(NB):
+            sb = str(b); c0 = L * b; end = t == NS - 1; cur[0] = b
+            B = lambda n: T[n + sb]
+            f0 = 2 * L * t; P_, F_, Z_ = B("pf")[:, f0:f0 + L], B("pf")[:, f0 + L:f0 + 2 * L], B("zz")[:]
+            pt_, ft_ = "P%s_%d" % (sb, t), "F%s_%d" % (sb, t)
+            gtok = ["gg%s_%d" % (sb, c) for c in range(GC)]
+            for c in range(GC):
+                act(B("gg")[:, 16 * LC * c:16 * LC * (c + 1)], T.gt[:].indirect(B("cu")[:, LC * c:LC * c + LC]), F.Identity,
+                    GT + ["cu" + sb], [gtok[c]], gather=True)
+            we = 768 if t == 0 else 768 + 192 * (t - 1) + c0 + L
+            act(B("mv")[:], B("mm")[:, 0:we].indirect(B("iy")[:, 0:W]), F.Identity,
+                ["m0_" + sb, "iy" + sb] + fills[b][t] + ["M%s_%d" % (sb, u) for u in range(t)], ["mv" + sb], gather=True)
+            mp = T["ps%d" % bk("m", b)]
+            for j in range(R): mm(bk("m", b), mp[:, j:R * L:R], [(Wt("I0"), B("mv")[:], ["I0", "mv" + sb], 1)])
+            pm("sc", b, [(T.b2[:, 15 - k:143 - k], B("gg")[:, k:16 * L:16], ["b2"] + gtok, 1) for k in range(16)], last=False)
+            pm("sc", b, [(Wt("WZS"), Z_, ["WZS", "zz" + sb], 1)], first=False, last=False)
+            for j in range(KS):
+                tt(B("ee")[:, j:16 * L:KS], B("gg")[:, j:16 * L:KS], mp[:, 0:R * L], A.is_equal, gtok, ["ee%s_%d" % (sb, j)], [bk("m", b)])
+            pm("sc", b, [(T.b1[:, 15 - k:143 - k], B("ee")[:, k:16 * L:16], ["b1", "ee%s_%d" % (sb, k % KS)], 1)
+                         for k in sorted(range(16), key=lambda k: k % KS)], first=False)
+            act(B("ok")[:], ps("sc", b), F.Relu, ["k1"], ["ok" + sb], bias=fc("k1"), scale=4096.0, banks=[bk("sc", b)])
+            o0 = 2 * L * (NB * t + b); om, of = (o0, o0 + L) if b < NB - 1 else (o0 + L, o0)
+            fi = T.outb[:, of:of + L]; ft = "fi%s_%d" % (sb, t)
+            pm("u", b, [(Wt("N4K"), B("cf")[:], ["N4K", "cf" + sb], 1), (Wt("TRI"), B("ok")[:], ["TRI", "ok" + sb], 1)])
+            if ON_S["cs"]: act(B("cs")[:], ps("u", b), F.Relu, ["k2"], ["cs" + sb], bias=fc("k2"), banks=[bk("u", b)])
+            else: ts(B("cs")[:], ps("u", b), -2048.0, 0.0, A.add, A.max, [], ["cs" + sb], banks=[bk("u", b)])
+            pm("cr", b, [(Wt("I0"), T.mc[:, 0:L], ["I0", "mc"], 1), (Wt("BLK"), B("cs")[:], ["BLK", "cs" + sb], 1)])
+            if ON_S["fi"]: act(fi, B("cs")[:], F.Sign, ["cs" + sb], [ft])
+            else: ts(fi, B("cs")[:], 1.0, None, A.min, None, ["cs" + sb], [ft], 0.5)
+            wrap(b, "cr", "sc", "ix", -1.0, 2048.0, A.mult, A.add)
+            ix = B("ix")[:, 0:W]; oc = slice(192 * t + c0, 192 * t + c0 + L); otk = "o%s_%d" % (sb, t); mtk = "M%s_%d" % (sb, t)
+            tt(B("bt")[:], T.zt[:].indirect(ix), B("mv")[:], A.max, ZT + ["ix" + sb, "mv" + sb], ["bt" + sb], gather=True)
+            tt(T.outb[:, om:om + L], T.pb[:].indirect(ix), B("bt")[:], A.min, PB + ["ix" + sb, "bt" + sb], [otk], gather=True)
+            l0 = 768 + 192 * t + lo(b)
+            land = B("mm")[:, l0 + of - o0:l0 + of - o0 + L]
+            fn, cnt = send(t, B("mm")[:, l0:l0 + 2 * L], T.outb[:, o0:o0 + 2 * L], "a%d_%d" % (b, t))
+            add("G", fn, [otk, ft], [mtk], 300.0, lat=COST["rem"] + (COST["rem0"] if t + b == 0 else 0.0), sem=("a%d_%d" % (b, t), cnt))
+            dma("Y", T.mn[:, oc], B("mm")[:, 768 + 192 * t + c0:768 + 192 * t + c0 + L], [mtk], [], 256 * L, False)
+            pm("fd", b, [(Wt("BLK"), fi, ["BLK", ft], 1)])
+            pm("P", b, [(Wt("WPP"), P_, ["WPP", pt_], 1), (Wt("WZP2"), Z_, ["WZP2", "zz" + sb], 1), (Wt("WFP"), fi, ["WFP", ft], 1)])
+            pm("F", b, [(Wt("WNN"), F_, ["WNN", ft_], 1), (Wt("WZN2"), Z_, ["WZN2", "zz" + sb], 1), (Wt("WFN"), fi, ["WFN", ft], 1)])
+            if not end:
+                tt(B("xx")[:], B("cf")[:], ps("fd", b), A.subtract, ["cf" + sb], ["xx" + sb], [bk("fd", b)])
+                tt(B("cf")[:], T.tc[:].indirect(ix), B("xx")[:], A.max, TC + ["ix" + sb, "xx" + sb], ["cf" + sb], gather=True)
+                ts(B("cu")[:], B("cf")[:], 4096.0, None, A.mult, None, ["cf" + sb], ["cu" + sb], 0.5)
+            t1 = B("t1")[:, L * t:L * t + L]; tk = "t1%s_%d" % (sb, t)
+            tt(t1, B("pd")[:], ps("fd", b), A.mult, ["pd" + sb], [tk], [bk("fd", b)])
+            f0 += 2 * L; P_, F_ = B("pf")[:, f0:f0 + L], B("pf")[:, f0 + L:f0 + 2 * L]
+            pt_, ft_ = "P%s_%d" % (sb, t + 1), "F%s_%d" % (sb, t + 1)
+            step01(B("pf")[:, f0:f0 + 2 * L], "P", b, 2, [pt_, ft_])
+            past[b] += [(Wt("WDT"), t1, ["WDT", tk], 1), (Wt("WDN"), F_, ["WDN", ft_], 1)]
+            pm("dq", b, past[b])
+            zt0 = [(Wt("WZZ"), Z_, zt_("WZZ") + ["zz" + sb], 1), (Wt("WZF"), fi, zt_("WZF") + [ft], 1),
+                   (Wt("WZC"), B("cs")[:], zt_("WZC") + ["cs" + sb], 1)]
+            zt1 = [(Wt("WZP"), P_, zt_("WZP") + [pt_], 1), (Wt("WZN"), F_, zt_("WZN") + [ft_], 1)]
+            zt2 = [(Wt("WZM"), land, zt_("WZM") + [mtk], 1)]
+            if not end:
+                look(b, t + 1)
+                zlayer(b, "zz", zt0 + zt1 + zt2)
+                continue
+            cp(B("pd")[:], DQ(b), [], ["pd" + sb], banks=[bk("dq", b)])
+            zlayer(b, "zp", zt0)
+            pm("m", b, [(Wt("I0"), T.tf[:, c0:c0 + L], ["I0", "tf"], 1), (Wt("LE"), B("pd")[:], ["LE", "pd" + sb], 1)])
+            pm("cr", b, [(Wt("I0"), T.mc[:, 0:L], ["I0", "mc"], 1), (Wt("WL"), B("zp")[:], ["WL", "zp" + sb], 1)])
+            wrap(b, "cr", "sx", "iy", -1.0, 2048.0, A.mult, A.add)
+            pm("sc", b, [(Wt("RR", 8), T.af[0:8, c0:c0 + L], ["RR", "af0"], 1), (Wt("WLX"), B("zp")[:], ["WLX", "zp" + sb], 1)])
+            pm("fi", b, [(Wt("BLK"), P_, ["BLK", pt_], 1)])
+            pm("xr", b, [(Wt("WW"), B("zp")[:], ["WW", "zp" + sb], 1)])
+            act(B("xx")[:], ps("sc", b), F.Identity, [], ["xx" + sb], banks=[bk("sc", b)])
+            act(T.ysb[:, 192 + c0:192 + c0 + L], ps("fi", b), F.Identity, ["k3"], ["yp" + sb], bias=fc("k3"), scale=-1.0, banks=[bk("fi", b)])
+            act(T.ysb[:, 576 + c0:576 + c0 + L], ps("xr", b), F.Identity, [], ["yw" + sb], banks=[bk("xr", b)])
+            tt(T.ysb[:, c0:c0 + L], T.gst[:].indirect(B("iy")[:, 0:W]), B("xx")[:], A.max,
+               ["gs%d" % c for c in range(4)] + ["iy" + sb, "xx" + sb], ["ys" + sb], gather=True)
+            pm("F", b, [(Wt("WNN"), F_, ["WNN", ft_], 1), (Wt("WZN2"), B("zp")[:], ["WZN2", "zp" + sb], 1), (Wt("BLK"), land, ["BLK", mtk], 1)])
+            ts(B("f2")[:], ps("F", b), 0.5, None, A.is_ge, None, [], ["f2" + sb], banks=[bk("F", b)])
+            tt(T.yqb[:, c0:c0 + L], B("f2")[:], ps("m", b), A.mult, ["f2" + sb], ["yq" + sb], [bk("m", b)])
+            dma("Y", T.yq[:, c0:c0 + L], T.yqb[:, c0:c0 + L], ["yq" + sb], [], 512 * L, False)
+            pm("yn", b, [(Wt("BLK"), F_, ["BLK", ft_], 1), (Wt("BLK"), land, ["BLK", mtk], 1)])
+            ts(T.ysb[:, 384 + c0:384 + c0 + L], ps("yn", b), 16.0, None, A.min, None, [], ["yn" + sb], banks=[bk("yn", b)])
+    dma("S", T.ys[:], T.ysb[0:128:16, :], [n + str(b) for n in ("ys", "yp", "yn", "yw") for b in range(NB)], [], 24576, False)
+    return ops
+
+
+GUESSES = [(1.0, 110.0, 70.0, 1.0, 0.0), (1.7, 110.0, 70.0, 1.0, 0.0), (1.0, 220.0, 140.0, 1.0, 0.0), (1.0, 110.0, 70.0, 1.4, 0.0),
+           (1.0, 60.0, 40.0, 0.7, 0.0), (1.0, 110.0, 70.0, 1.0, 50.0)]
+ORDER = {}
+
+
+def schedule(ops):
+    n = len(ops)
+    if n in ORDER: return ORDER[n]
+    pre = [[] for _ in range(n)]
+    suc = [[] for _ in range(n)]
+    for i, o in enumerate(ops):
+        for j in o["dep"] | o["ord"]:
+            gap = 0.0
+            if j in o["dep"]: gap = ops[j]["lat"] + (COST["self"] if ops[j]["e"] == o["e"] else COST["hop"])
+            pre[i].append((j, gap)); suc[j].append((i, gap))
+    cost = [o["c"] for o in ops]
+
+    def sweep(order, before, head):
+        busy, fin = {}, [0.0] * n
+        for i in order:
+            s = head[i]
+            for j, gap in before[i]:
+                if fin[j] + gap > s: s = fin[j] + gap
+            a, b = busy.setdefault(ops[i]["e"], ([], []))
+            lo, hi = 0, len(b)
+            while lo < hi:
+                mid = (lo + hi) // 2
+                if b[mid] > s: hi = mid
+                else: lo = mid + 1
+            k = lo
+            while k < len(a) and a[k] < s + cost[i]:
+                s = max(s, b[k]); k += 1
+            a.insert(k, s); b.insert(k, s + cost[i]); fin[i] = s + cost[i]
+        return fin
+
+    def length(seq):
+        total = 0.0
+        for pe, hop, own, rem, extra in GUESSES:
+            free, fin = {}, [0.0] * n
+            for i in seq:
+                o = ops[i]; e = o["e"]; s = free.get(e, 0.0)
+                for j in o["dep"]:
+                    ej = ops[j]["e"]
+                    r = fin[j] + ops[j]["lat"] * (rem if ej == "G" else 1.0) + (own if ej == e else hop)
+                    if r > s: s = r
+                fin[i] = free[e] = s + cost[i] * (pe if e == "P" else 1.0) + (extra if e in "VS" else 0.0)
+            total += max(fin[i] + ops[i]["lat"] for i in range(n))
+        return total
+    zero = [0.0] * n
+    tail = [o["lat"] for o in ops]
+    best = None
+    rnd = np.random.RandomState(COST["seed"])
+    for skew in COST["skews"]:
+        prio = [0.0] * n
+        for i in range(n - 1, -1, -1):
+            prio[i] = cost[i] + max([tail[i]] + [gap + prio[k] for k, gap in suc[i]])
+        key = [-(prio[i] - skew * ops[i]["b"]) for i in range(n)]
+        for i in range(n):
+            for j, gap in pre[i]: key[i] = max(key[i], key[j] + 1e-3)
+        for it in range(COST["rounds"]):
+            fin = sweep(sorted(range(n), key=lambda i: key[i]), pre, zero)
+            seq = sorted(range(n), key=lambda i: (fin[i] - cost[i], i))
+            end = length(seq)
+            if best is None or end < best[0]: best = (end, seq, fin)
+            noise = rnd.rand(n) * COST["noise"]
+            key = [-fin[i] + noise[i] for i in range(n)]
+            for i in range(n - 1, -1, -1):
+                for k, gap in suc[i]: key[i] = max(key[i], key[k] + 1e-3)
+            back = sweep(sorted(range(n), key=lambda i: key[i]), suc, tail)
+            noise = rnd.rand(n) * COST["noise"]
+            key = [-back[i] + noise[i] for i in range(n)]
+            for i in range(n):
+                for j, gap in pre[i]: key[i] = max(key[i], key[j] + 1e-3)
+    ORDER[n] = (best[1], best[2])
+    return ORDER[n]
+
+
+def rank_program(g, core, T, topo):
+    rank = T.rank_of(core)
+    if rank is None:
+        return
+    cores = T.cores
+    n = len(cores)
+
+    def common(c):
+        m = -1
+        for d in cores:
+            if d != c: m &= topo.mask(c, d)
+        return m
+    total = [0]
+
+    def send(t, land, src, sem):
+        d = 1 + t % (n - 1)
+        dst = cores[(rank + d) % n]
+        rid, pid = topo.addr(dst, core)
+        m = common(core)
+        total[0] += bin(m).count("1")
+        return (lambda: g.remote_dma(land, src, T.sem[sem], T.sem.sent, pid, rid, m)), bin(common(cores[(rank - d) % n])).count("1")
+
+    ops = build(g, T, send)
+    seq, fin = schedule(ops)
+    need = set()
+    for o in ops: need.update(o["dep"])
+    queue = {"V": g.vector, "S": g.scalar, "P": g.tensor, "G": g, "Y": g.sync}
+    count, mark, seen, waited = {}, {}, {}, {}
+    for i in seq:
+        o = ops[i]; q = queue[o["e"]]
+        want = {}
+        for j in o["dep"]:
+            s, v = mark[j]
+            want[s] = max(want.get(s, 0), v)
+        for s, v in want.items():
+            if seen.get((o["e"], s), 0) < v:
+                q.wait_ge(T.sem[s], v); seen[(o["e"], s)] = v; waited[s] = max(waited.get(s, 0), v)
+        ins = o["fn"]()
+        if o["sem"]:
+            mark[i] = o["sem"]; count[o["sem"][0]] = o["sem"][1]
+            if o["e"] != "G": ins.then_inc(T.sem[o["sem"][0]], 16)
+        elif i in need:
+            s = "c" + o["e"]; count[s] = count.get(s, 0) + 1; mark[i] = (s, count[s])
+            ins.then_inc(T.sem[s], 1)
+    g.wait_ge(T.sem.sent, total[0])
+    for s, v in count.items():
+        if waited.get(s, 0) < v: g.sync.wait_ge(T.sem[s], v)

@@ -1,413 +1,419 @@
 import numpy as np
+from concourse.bass import DstId, RemoteDMATransfer
 from concourse.mybir import AluOpType as A, ActivationFunctionType as F
 
 NB = 3
 L = 192 // NB
 W = L // 16
 R = 4
-GC = 2
+PIECES = [("S", 0, L // 2), ("S", L // 2, L)]
 KEEP = (1, 3)
+ON = {"ok": "V", "cs": "S", "pg": "S", "mv": "S", "dq": "S", "mn": "V", "tc": "V", "pb": "S", "cf": "G", "fold": False}
 H16 = "float16"
 NS = 6
 BIG = float(2 ** 40)
-ON_S = {"cs": True, "fi": True, "pf": True}
-WN = ["BLK", "I0", "I40", "LE", "TRI", "WPP", "WNN", "WDT", "WDN", "WFP", "WFN", "N4K", "WZS", "WZP2",
-      "WZN2", "WL", "WLX", "WW", "NBL", "RR", "WZZ", "WZF", "WZC", "WZP", "WZN", "WZM"]
+ONE, RS, A3, A4, WR, L5, L6, PR, NR = 0, 1, 3, 4, 9, 10, 11, 12, 13
+WN = ["BLK", "I0", "NI", "DD", "SS", "LE", "TRI", "WDT", "WDN", "NBD", "RR", "WZA", "WZ2", "WZB", "WZZ", "WZF", "WZC", "WZP", "WZG", "WZM",
+      "WL", "WLX", "WW", "X0", "YB"]
 
 SCRATCH = {
     "ptb": ("sbuf", [128, 2048], "bfloat16"), "fl": ("sbuf", [128, 2048], "bfloat16"), "gt": ("sbuf", [128, 2048], "bfloat16"),
-    "clb": ("sbuf", [128, 1280], "int32"), "xb": ("sbuf", [128, 256], "int32"), "xf": ("sbuf", [128, 256], "float32"),
-    "bw": ("sbuf", [128, 256], "uint16"), "pb": ("sbuf", [128, 2064], "bfloat16"), "zt": ("sbuf", [128, 2064], "bfloat16"),
-    "tc": ("sbuf", [128, 2056], "float32"), "gst": ("sbuf", [128, 2056], "int32"),
+    "clb": ("sbuf", [128, 2056], "int32"), "xb": ("sbuf", [128, 256], "int32"), "xh": ("sbuf", [128, 256], H16),
+    "xt": ("sbuf", [128, 256], H16), "bw": ("sbuf", [128, 256], "uint16"),
+    "pb": ("sbuf", [128, 2240], "bfloat16"), "zt": ("sbuf", [128, 2240], "bfloat16"), "tc": ("sbuf", [128, 2240], "float32"),
+    "mm": ("sbuf", [128, 1920], "bfloat16"), "mo": ("sbuf", [128, 1152], "bfloat16"), "outb": ("sbuf", [128, 1152], "bfloat16"),
+    "outa": ("sbuf", [128, 1152], "bfloat16"),
     "ai": ("sbuf", [128, 768], "int32"), "af": ("sbuf", [128, 768], H16), "qi": ("sbuf", [128, 192], "int32"),
-    "qa": ("sbuf", [128, 192], "float32"), "top": ("sbuf", [128, 192], "float32"), "jr": ("sbuf", [128, 192], "float32"),
-    "jb": ("sbuf", [128, 128], "float32"), "jf": ("sbuf", [128, 144], "float32"),
-    "i32": ("sbuf", [128, 128], "float32"), "ic": ("sbuf", [128, 8], "int32"),
-    "fc": ("sbuf", [128, 32], "float32"), "oh": ("sbuf", [128, 16], "float32"),
-    "b1": ("sbuf", [128, 144], "bfloat16"), "b2": ("sbuf", [128, 144], "bfloat16"),
-    "wt": ("sbuf", [128, 128 * len(WN)], "bfloat16"),
-    "mc": ("sbuf", [128, 192], "bfloat16"), "mx": ("sbuf", [128, 192], H16), "rs": ("sbuf", [128, 192], "float32"),
-    "tf": ("sbuf", [128, 192], H16), "dg": ("sbuf", [128, 192], "float32"), "e0": ("sbuf", [128, 192], H16),
-    "outb": ("sbuf", [128, 2304], "bfloat16"),
+    "qa": ("sbuf", [128, 192], H16), "top": ("sbuf", [128, 192], "float32"), "f0": ("sbuf", [128, 192], H16),
+    "jr": ("sbuf", [128, 192], "bfloat16"), "jb": ("sbuf", [128, 128], "bfloat16"), "j1": ("sbuf", [128, 128], "bfloat16"),
+    "jf": ("sbuf", [128, 160], "bfloat16"), "ic": ("sbuf", [128, 8], "int32"),
+    "fc": ("sbuf", [128, 40], "float32"), "oh": ("sbuf", [128, 16], "float32"),
+    "b1": ("sbuf", [128, 160], "bfloat16"), "b2": ("sbuf", [128, 160], "bfloat16"),
+    "ie": ("sbuf", [128, 160], H16), "iod": ("sbuf", [128, 160], H16),
+    "wt": ("sbuf", [128, 128 * len(WN)], H16),
+    "mc": ("sbuf", [128, 192], H16), "mx": ("sbuf", [128, 192], H16), "dg": ("sbuf", [128, 192], H16),
+    "rs": ("sbuf", [128, 192], "float32"), "r0": ("sbuf", [128, 192], "float32"), "r2": ("sbuf", [128, 192], "float32"),
+    "tf": ("sbuf", [128, 192], H16), "e0": ("sbuf", [128, 192], H16), "s1": ("sbuf", [128, 192], "float32"),
+    "i0": ("sbuf", [128, 16], "uint16"), "zp": ("sbuf", [128, 192], H16),
     "yqb": ("sbuf", [128, 192], "float32"), "ysb": ("sbuf", [128, 768], "float32"),
 }
 for _b in range(NB):
-    for _n, _s, _d in (("mm", [128, 1920], "bfloat16"), ("gg", [128, 16 * L], "bfloat16"), ("ee", [128, 16 * L], "bfloat16"),
-                       ("cf", [128, L], H16), ("cu", [128, L], "uint16"), ("xx", [128, L], "float32"),
-                       ("ok", [128, L], "bfloat16"), ("cs", [128, L], H16),
-                       ("sc", [128, L], "float32"), ("sx", [128, L], "float32"), ("ix", [128, 16], "uint16"),
-                       ("iy", [128, 16], "uint16"), ("mv", [128, L], "bfloat16"), ("bt", [128, L], "bfloat16"),
-                       ("pf", [128, 14 * L], "bfloat16"), ("t1", [128, 6 * L], H16), ("pd", [128, L], H16), ("dq", [128, L], H16),
-                       ("zz", [128, L], H16), ("zp", [128, L], H16), ("f2", [128, L], "bfloat16")):
-        SCRATCH[_n + str(_b)] = ("sbuf", _s, _d)
+    for _n, _s, _d in (("gg", 16 * L, "bfloat16"), ("ee", 16 * L, "bfloat16"), ("cu", L, "uint16"), ("xx", L, "float32"),
+                       ("ok", L, H16), ("cs", 2 * L, H16), ("sc", L, "float32"), ("sx", L, "float32"), ("ix", 16, "uint16"),
+                       ("iy", 16, "uint16"), ("mv", L, "bfloat16"), ("bt", L, "bfloat16"), ("pg", 14 * L, H16),
+                       ("t1", 6 * L, H16), ("pd", L, H16), ("cf", L, H16), ("dq", L, H16), ("zz", L, H16), ("f2", L, H16)):
+        SCRATCH[_n + str(_b)] = ("sbuf", [128, _s], _d)
 for _b in range(8):
     SCRATCH["ps" + str(_b)] = ("psum", [128, 512], "float32")
 
-SEMAPHORES = (["cV", "cS", "cP", "cG", "sent"] + ["d%d" % _i for _i in range(60)]
+SEMAPHORES = (["cV", "cS", "cP", "cG", "sent"] + ["d%d" % _i for _i in range(40)]
               + ["a%d_%d" % (_b, _t) for _b in range(NB) for _t in range(NS)])
 
-COST = {"cy": 1.0, "v0": 25.0, "s0": 70.0, "g": 1.56, "pe": 0.5, "hop": 140.0, "self": 85.0, "rem": 2600.0, "rem0": 2500.0,
-        "dma": 1900.0, "bw": 230.0, "skews": [1500.0, 2400.0, 3300.0], "rounds": 100, "noise": 150.0, "seed": 1}
+COST = {"cy": 0.9, "v0": 20.0, "s0": 75.0, "g": 1.6, "pe": 0.58, "hop": 130.0, "self": 130.0, "rem": 2500.0, "rem0": 2800.0,
+        "dma": 1500.0, "bw": 200.0, "skews": [1200.0, 2000.0, 2800.0], "rounds": 150, "noise": 150.0, "seed": 1}
 
-
-def place(name, b):
-    if NB == 2:
-        bank, reg = {"m": (0, 0), "sc": (1, 0), "fi": (1, 1), "cr": (1, 2), "xr": (1, 3), "yn": (1, 4), "fd": (2, 0),
-                     "P": (2, 2), "F": (2, 3), "u": (2, 4), "z": (2, 4), "dq": (6 + b, 0)}[name]
-        return (bank, reg) if bank > 5 else (3 * b + bank, reg)
-    bank, reg = {"m": (0, 0), "fd": (0, 4), "P": (0, 6), "F": (0, 7), "sc": (1, 0), "fi": (1, 1), "cr": (1, 2),
-                 "xr": (1, 3), "yn": (1, 4), "u": (1, 5), "z": (6 + b % 2, b), "dq": (1, 6)}[name]
-    return (bank, reg) if bank > 5 else (2 * b + bank, reg)
+PLACE = {"m": (0, 0), "u": (0, 4), "fi": (0, 5), "P": (0, 6), "G": (0, 7), "dq": (0, 4), "xr": (0, 5),
+         "sc": (1, 0), "cr": (1, 1), "fd": (1, 2), "y1": (1, 3), "y2": (1, 4), "y3": (1, 5), "z": (6, 0)}
 
 
 def build(g, T, send):
     ops, wr, rd, bank, cur = [], {}, {}, {}, [0]
     cy = COST["cy"]
 
-    def add(eng, fn, reads, writes, cost, banks=(), lat=0.0, sem=None):
+    def v(name, a=0, b=None, s=1, p=None):
+        t = T[name]
+        if b is None: b = t.shape[1]
+        m = 0
+        if s == 1: m = ((1 << (b - a)) - 1) << a
+        else:
+            for c in range(a, b, s): m |= 1 << c
+        return (t[p if p else slice(0, 128), slice(a, b, s) if s > 1 else slice(a, b)], [(name, m)])
+
+    def ind(win, off): return (win[0].indirect(off[0]), win[1] + off[1])
+    ap = lambda x: x[0] if isinstance(x, tuple) else x
+
+    def add(eng, fn, ins, outs, cost, lat=0.0, sem=None, chain=None):
         i = len(ops)
         dep, order = set(), set()
-        for t in reads:
-            if t in wr: dep.add(wr[t])
-        for t in writes:
-            if t in wr: dep.add(wr[t])
-            dep.update(rd.get(t, ()))
+        reads = [k for x in ins if isinstance(x, tuple) for k in x[1]]
+        writes = [k for x in outs for k in x[1]]
+        banks = set(n for n, m in reads + writes if n[:2] == "ps")
+        if chain: banks.add(chain)
         for b in banks:
             last = bank.setdefault(b, {})
             for e, j in last.items():
                 if e != eng: dep.add(j)
                 else: order.add(j)
             last[eng] = i
-        for t in reads: rd.setdefault(t, []).append(i)
-        for t in writes:
-            wr[t] = i; rd[t] = []
+        for n, m in reads:
+            if n in banks: continue
+            dep.update(j for k, j in wr.get(n, ()) if k & m)
+        for n, m in writes:
+            if n in banks: continue
+            dep.update(j for k, j in wr.get(n, ()) if k & m)
+            dep.update(j for k, j in rd.get(n, ()) if k & m)
+            wr[n] = [(k & ~m, j) for k, j in wr.get(n, ()) if k & ~m] + [(m, i)]
+            rd[n] = [(k & ~m, j) for k, j in rd.get(n, ()) if k & ~m]
+        for n, m in reads:
+            if n not in banks: rd.setdefault(n, []).append((m, i))
         dep.discard(i)
-        ops.append({"e": eng, "fn": fn, "dep": dep, "ord": order, "c": cost, "lat": lat, "sem": sem, "b": cur[0], "w": writes})
-        return i
+        ops.append({"e": eng, "fn": fn, "dep": dep, "ord": order, "c": cost, "lat": lat, "sem": sem, "b": cur[0]})
 
-    def n_of(ap):
-        n = 1
-        for s in ap.shape[1:]: n *= s
-        return n
+    n_of = lambda x: x[0].shape[1]
+    gath = lambda x: len(x[1]) > 1
+    two = lambda *xs: all(SCRATCH[x[1][0][0]][2] in ("bfloat16", H16, "uint16") for x in xs)
+    psum = lambda x: x[1][0][0][:2] == "ps"
 
-    def vcost(n, f): return COST["v0"] + max(64.0, n * f) * cy
+    def vcost(out, in0, f):
+        if gath(in0): return 60.0 + n_of(out) * COST["g"] * cy
+        return COST["v0"] + max(64.0, n_of(out) * f) * cy
 
-    def ts(out, in0, s1, s2, op0, op1, r, w, f=1.0, banks=(), gather=False):
-        if op1 is None: fn = lambda: g.vector.tensor_scalar(out, in0, s1, None, op0)
-        else: fn = lambda: g.vector.tensor_scalar(out, in0, s1, s2, op0, op1)
-        add("V", fn, r, w, 50.0 + n_of(out) * COST["g"] * cy if gather else vcost(n_of(out), f), banks)
+    def ts(out, in0, s1, s2, op0, op1=None):
+        if op1 is None: fn = lambda: g.vector.tensor_scalar(out[0], in0[0], ap(s1), None, op0)
+        else: fn = lambda: g.vector.tensor_scalar(out[0], in0[0], ap(s1), ap(s2), op0, op1)
+        add("V", fn, [in0, s1, s2], [out], vcost(out, in0, 0.5 if two(out, in0) else 1.0))
 
-    def tt(out, in0, in1, op, r, w, banks=(), gather=False):
-        n = n_of(out)
-        c = 50.0 + n * COST["g"] * cy if gather else vcost(n, 1.0 if banks else 2.0)
-        add("V", lambda: g.vector.tensor_tensor(out, in0, in1, op), r, w, c, banks)
+    def tt(out, in0, in1, op):
+        add("V", lambda: g.vector.tensor_tensor(out[0], in0[0], in1[0], op), [in0, in1], [out],
+            vcost(out, in0, 1.0 if psum(in0) or psum(in1) else 2.0))
 
-    def cp(out, in_, r, w, f=1.0, banks=(), gather=False):
-        n = n_of(out)
-        add("V", lambda: g.vector.tensor_copy(out, in_), r, w, 50.0 + n * COST["g"] * cy if gather else vcost(n, f), banks)
+    def cp(out, in_):
+        add("V", lambda: g.vector.tensor_copy(out[0], in_[0]), [in_], [out], vcost(out, in_, 0.5 if two(out, in_) else 1.0))
 
-    def act(out, in_, func, r, w, bias=0.0, scale=1.0, banks=(), gather=False, extra=0.0):
-        c = COST["s0"] + n_of(out) * cy * (COST["g"] if gather else 1.0) + extra
-        add("S", lambda: g.scalar.activation(out, in_, func, bias=bias, scale=scale), r, w, c, banks)
+    def scan(out, d0, d1, init):
+        add("V", lambda: g.vector.tensor_tensor_scan(out[0], d0[0], d1[0], init, A.min, A.max), [d0, d1], [out], vcost(out, d0, 1.0))
 
-    def mm(b, out, terms, first=True, last=True):
-        for j, (lh, rh, r, k) in enumerate(terms):
+    once = [1300.0]
+
+    def act(out, in_, func, bias=0.0, scale=1.0):
+        c = COST["s0"] + n_of(out) * cy * (COST["g"] if gath(in_) else 1.0)
+        if func == F.Sigmoid: c += once[0]; once[0] = 0.0
+        add("S", lambda: g.scalar.activation(out[0], in_[0], func, bias=ap(bias), scale=ap(scale)), [in_, bias, scale], [out], c)
+
+    def move(q, out, in_):
+        if q == "S": act(out, in_, F.Identity)
+        else: cp(out, in_)
+
+    def mm(out, terms, first=True, last=True):
+        for j, term in enumerate(terms):
+            lh, rh = term[:2]; o = term[2] if len(term) > 2 else out
             st, sp = first and j == 0, last and j == len(terms) - 1
-            add("P", lambda lh=lh, rh=rh, st=st, sp=sp: g.tensor.matmul(out, lh, rh, st, sp), r, [],
-                max(64.0, n_of(rh)) * COST["pe"] * k, [b])
+            add("P", lambda o=o, lh=lh, rh=rh, st=st, sp=sp: g.tensor.matmul(o[0], lh[0], rh[0], st, sp), [lh, rh], [o],
+                max(64.0, n_of(rh)) * COST["pe"] * (1 if two(rh) else 4))
 
-    def iota(out, pat, base, mul, w, fl=True):
-        if fl: fn = lambda: g.iota(out, pat, base, mul, allow_small_or_imprecise_dtypes=True)
-        else: fn = lambda: g.iota(out, pat, base, mul)
-        add("G", fn, [], w, 130.0 + 2 * n_of(out) * cy)
+    def iota(out, pat, base, mul=0):
+        if SCRATCH[out[1][0][0]][2] == "int32": fn = lambda: g.iota(out[0], pat, base, mul)
+        else: fn = lambda: g.iota(out[0], pat, base, mul, allow_small_or_imprecise_dtypes=True)
+        add("G", fn, [], [out], 130.0 + 2 * n_of(out) * cy)
 
-    def fill(out, v, w, fl=True): iota(out, [[0, n_of(out)]], v, 0, w, fl)
+    def fill(out, val): iota(out, [[0, n_of(out)]], val)
 
-    def band(n, src, sign, base, op, other):
-        add("G", lambda: g.affine_select(Wt(n), Wt(src), [[sign, 128]], op, other, base, -sign), [src], [n], 170.0 + 256 * cy)
+    def band(n, src, pat, mul, base, op, other):
+        add("G", lambda: g.affine_select(Wt(n)[0], Wt(src)[0], pat, op, other, base, mul), [Wt(src)], [Wt(n)], 170.0 + 256 * cy)
 
     nd, queued = [0], [0.0]
 
-    def dma(q, out, in_, r, w, nbytes, load=True):
+    def dma(q, out, in_, nbytes, load=True):
         s = "d%d" % nd[0]; nd[0] += 1
         eng = g.sync if q == "Y" else g.scalar
         if load: queued[0] += nbytes / COST["bw"]
         lat = COST["dma"] + (queued[0] if load else nbytes / COST["bw"])
-        add(q, lambda: eng.dma_start(out, in_), r, w, 60.0, lat=lat, sem=(s, 16), banks=["q" + q] if load else [])
+        add(q, lambda: eng.dma_start(ap(out), ap(in_)), [in_], [out] if isinstance(out, tuple) else [], 60.0, lat, (s, 16),
+            "load" if load else None)
 
-    def Wt(n, rows=128):
-        j = WN.index(n)
-        return T.wt[0:rows, 128 * j:128 * j + 128]
-
-    def Wc(n, r):
-        j = WN.index(n)
-        return T.wt[:, 128 * j + r:128 * j + 128:16]
+    def Wt(n, p=None): return v("wt", 128 * WN.index(n), 128 * WN.index(n) + 128, 1, p)
+    def Wc(n, r, s=16): return v("wt", 128 * WN.index(n) + r, 128 * WN.index(n) + 128, s)
 
     def ps(name, b, n=1):
-        k, a = place(name, b)
-        return T["ps%d" % k][:, a * L:(a + n) * L]
+        k, a = PLACE[name]
+        if k == 6: k, a = 6 + b % 2, b
+        else: k += 2 * b
+        return v("ps%d" % k, a * L, (a + n) * L)
 
-    bk = lambda name, b: place(name, b)[0]
-    DQ = lambda b: ps("dq", b)
+    top8 = slice(0, 8)
+    row0 = slice(0, 128, 16)
 
-    def pm(name, b, terms, first=True, last=True): mm(bk(name, b), ps(name, b), terms, first, last)
-
+    dma("Y", v("xb", 0, 128), T.bo[:], 65536)
     for j, n in enumerate(("s0", "p0", "n0", "w0")):
-        dma("S", T.ai[0:8, 192 * j:192 * j + 192], T[n][:], [], ["ai%d" % j], 6144)
-    for k in range(8):
-        dma("S", T.xb[:, 16 * k:16 * k + 16], T.bo[k, :], [], ["xb%d" % k], 16384)
-    for h in range(2):
-        dma("Y", T.ptb[:, 1024 * h:1024 * h + 1024], T.pt[:, 1024 * h:1024 * h + 1024], [], ["pt%d" % h], 262144)
-    dma("S", T.qi[:], T.q0[:], [], ["qi"], 98304)
-    for k in range(8):
-        dma("Y", T.xb[:, 128 + 16 * k:144 + 16 * k], T.gs[k, :], [], ["xb%d" % (8 + k)], 16384)
-    dma("Y", T.clb[:], T.cl[:], [], ["cl"], 655360)
-    dma("Y", T.mm0[:, 0:768], T.m0[:], [], ["m0_0"], 196608)
-    for b in range(1, NB):
-        dma("Y", T["mm%d" % b][:, 0:768], T.m0[:], [], ["m0_%d" % b], 196608)
+        dma("Y", v("ai", 192 * j, 192 * j + 192, 1, top8), T[n][:], 6144)
+    for c in range(2): dma("Y", v("ptb", 1024 * c, 1024 * c + 1024), T.pt[:, 1024 * c:1024 * c + 1024], 262144)
+    dma("Y", v("clb", 0, 1280), T.cl[:], 655360)
+    dma("Y", v("qi"), T.q0[:], 98304)
+    dma("Y", v("mm", 0, 768), T.m0[:], 196608)
+    dma("Y", v("xb", 128, 256), T.gs[:], 65536)
 
-    names = ["g16", "x", "p16", "f1", "f2", "f5", "c1", "c2", "hi", "f23", "f40", "fp", "xm", "xn", "u0", "u1", "u2", "u3", "u4",
-             "k0", "k1", "k2", "k3", "k4", "k5"]
-    fc = lambda n: T.fc[:, names.index(n):names.index(n) + 1]
-    oh = lambda k: T.oh[:, k:k + 1]
-    iota(T.ic[:, 0:1], [[1, 1]], 0, 1, ["p"], False)
-    iota(T.jb[:], [[16, 8], [0, 16]], 0, 0, ["jb"])
-    iota(T.jr[:], [[0, 12], [1, 16]], 0, 0, ["jr"])
-    iota(T.rs[:, 0:L], [[0, W], [4096, 16]], 0, 0, ["rs"])
-    iota(T.jf[:], [[1, 144]], -15, 0, ["jf"])
-    iota(T.top[:], [[1, 192]], 576, 0, ["top"])
-    iota(T.dg[:], [[1, 192]], 1600, 0, ["dg"])
-    iota(fc("p16"), [[1, 1]], 0, 16, ["p16"])
-    for c in range(4): fill(T.gst[:, 514 * c:514 * c + 514], -1, ["gs%d" % c], False)
-    dma("Y", T.gst[0:128:16, 0:2048], T.gs[:], [], ["gs%d" % c for c in range(4)], 65536, False)
-    ts(T.ic[:, 1:2], T.ic[:, 0:1], 112, None, A.bitwise_and, None, ["p"], ["ic1"])
-    ts(T.ic[:, 2:3], T.ic[:, 0:1], 15, None, A.bitwise_and, None, ["p"], ["ic2"])
-    cp(T.fc[:, 0:2], T.ic[:, 1:3], ["ic1", "ic2"], ["g16", "x"])
-    ts(Wt("BLK"), T.jb[:], fc("g16"), None, A.is_equal, None, ["jb", "g16"], ["BLK"])
-    ts(Wt("RR", 8), T.jb[0:8, :], T.fc[0:8, 2:3], None, A.is_equal, None, ["jb", "p16"], ["RR"])
-    ts(T.b1[:], T.jf[:], fc("g16"), None, A.is_equal, None, ["jf", "g16"], ["b1"])
-    act(T.b2[:], T.b1[:], F.Identity, ["b1"], ["b2"], scale=1.0 / BIG)
-    band("I0", "BLK", 1, 0, A.is_equal, 0.0)
-    act(Wt("I40"), Wt("I0"), F.Identity, ["I0"], ["I40"], scale=BIG)
-    act(T.i32[:], Wt("I0"), F.Identity, ["I0"], ["i32"], scale=-1.0)
-    act(Wt("N4K"), Wt("I0"), F.Identity, ["I0"], ["N4K"], scale=-4096.0)
-    act(Wt("NBL"), Wt("BLK"), F.Identity, ["BLK"], ["NBL"], scale=-1.0)
-    band("WDT", "BLK", 1, 1, A.is_equal, 0.0); band("WDT", "WDT", 1, 0, A.not_equal, -1.0)
-    band("TRI", "NBL", 1, 0, A.is_gt, 0.0); band("TRI", "TRI", 1, 0, A.not_equal, 1.0)
-    band("WPP", "BLK", 1, 0, A.is_ge, 0.0); band("WPP", "WPP", -1, 1, A.is_ge, 0.0)
-    band("WNN", "BLK", 1, 1, A.is_ge, 0.0); band("WNN", "WNN", -1, 1, A.is_ge, 0.0)
-    band("LE", "BLK", -1, 0, A.is_ge, 0.0)
-    act(Wt("WDN"), Wt("WDT"), F.Identity, ["WDT"], ["WDN"], scale=192.0)
-    act(Wt("WFP"), Wt("BLK"), F.Identity, ["BLK"], ["WFP"], scale=3.0)
-    act(Wt("WFN"), Wt("BLK"), F.Identity, ["BLK"], ["WFN"], scale=-1.0)
-    act(Wc("WFN", 15), Wc("BLK", 0), F.Identity, ["BLK"], ["WFN"], scale=-2.0)
-    ts(T.oh[:], T.jr[:, 0:16], fc("x"), None, A.is_equal, None, ["jr", "x"], ["oh"])
+    names = ["g16", "x", "h", "p", "p16", "g32", "a32", "s32", "pe", "po", "u0", "f1", "f2", "f5", "u1", "hi", "fp", "xm", "fa", "fb", "fn",
+             "thr", "sb", "k1", "k2", "k3", "k4"]
+    fc = lambda n: v("fc", names.index(n), names.index(n) + 1)
+    oh = lambda k: v("oh", k, k + 1)
+    iota(v("ic", 0, 1), [[1, 1]], 0, 1)
+    iota(fc("p"), [[1, 1]], 0, 1)
+    iota(v("jf"), [[1, 160]], -16)
+    iota(v("jb"), [[16, 8], [0, 16]], 0)
+    iota(v("j1"), [[32, 8], [1, 16]], 0)
+    iota(v("jr"), [[0, 12], [1, 16]], 0)
+    iota(fc("p16"), [[1, 1]], 0, 16)
+    for j, bits in enumerate((112, 15, 16)): ts(v("ic", 1 + j, 2 + j), v("ic", 0, 1), bits, None, A.bitwise_and)
+    cp(v("fc", 0, 3), v("ic", 1, 4))
+    ts(fc("pe"), fc("h"), 64.0, fc("p"), A.mult, A.add)
+    ts(fc("u0"), fc("h"), -64.0, 1024.0, A.mult, A.add)
+    ts(fc("po"), fc("u0"), fc("p"), None, A.add)
+    ts(v("ie"), v("jf"), fc("pe"), None, A.is_equal)
+    ts(v("iod"), v("jf"), fc("po"), None, A.is_equal)
+    ts(Wt("BLK"), v("jb"), fc("g16"), None, A.is_equal)
+    ts(Wt("RR", top8), v("jb", 0, 128, 1, top8), v("fc", names.index("p16"), names.index("p16") + 1, 1, top8), None, A.is_equal)
+    ts(v("b1"), v("jf"), fc("g16"), -0.5, A.is_equal, A.mult)
+    ts(v("b2"), v("jf"), fc("g16"), -0.5 / BIG, A.is_equal, A.mult)
+    act(fc("g32"), fc("g16"), F.Identity, scale=2.0)
+    act(fc("a32"), fc("g16"), F.Identity, bias=fc("p"))
+    act(fc("s32"), fc("x"), F.Identity, scale=-1.0, bias=fc("g32"))
+    ts(Wt("DD"), v("j1"), fc("a32"), None, A.subtract)
+    ts(Wt("SS"), v("j1"), fc("s32"), None, A.subtract)
+    ts(Wt("YB"), v("j1"), fc("g32"), None, A.subtract)
+    ts(Wt("I0"), Wt("DD"), 0.0, None, A.is_equal)
+    act(Wt("NI"), Wt("I0"), F.Identity, scale=-1.0)
+    diag = ([[1, 128]], -1, 0)
+    ts(Wt("WDT"), Wt("DD"), -1.0, -1.0, A.is_equal, A.mult); band("WDT", "WDT", *diag, A.not_equal, 1.0)
+    ts(Wt("WDN"), Wt("SS"), 14.0, 192.0, A.is_equal, A.mult); band("WDN", "WDN", [[-16, 8], [1, 16]], 1, -15, A.not_equal, -192.0)
+    act(Wt("TRI"), Wt("BLK"), F.Identity, scale=-4096.0)
+    band("TRI", "TRI", *diag, A.is_gt, 0.0); band("TRI", "TRI", *diag, A.not_equal, 4096.0)
+    act(Wt("NBD"), Wt("BLK"), F.Identity, scale=-1.0 / 2048)
+    ts(v("oh"), v("jr", 0, 16), fc("x"), None, A.is_equal)
 
     def col(n, k, c, prev):
-        act(fc(n), oh(k), F.Identity, ["oh"] + ([prev] if isinstance(prev, str) else []), [n], scale=c,
-            bias=oh(prev) if isinstance(prev, int) else fc(prev))
-    col("u0", 3, 16.0, 1); col("u1", 2, 128.0, "u0"); col("f1", 0, -128.0, "u1")
-    ts(fc("f2"), oh(0), 40.0, fc("f1"), A.mult, A.subtract, ["oh", "f1"], ["f2"])
-    col("f5", 5, 1.0, 6); col("c1", 2, -1.0, 1); col("u2", 2, 40.0, 0); col("c2", 3, -17.0, "u2")
-    col("u3", 1, 1.0, "f5"); ts(fc("hi"), fc("u3"), 4095.0, 1.0, A.mult, A.add, ["u3"], ["hi"])
-    col("f23", 2, 1.0, 3); col("f40", 0, -1.0, 4)
-    ts(fc("fp"), oh(15), 1.0, None, A.add, None, ["oh"], ["fp"])
-    act(fc("u4"), oh(0), F.Identity, ["oh"], ["u4"], scale=-17.0)
-    ts(fc("xm"), fc("x"), -15.0, None, A.add, None, ["x"], ["xm"])
-    act(fc("xn"), fc("xm"), F.Identity, ["xm"], ["xn"], scale=-1.0)
-    ts(fc("k4"), fc("x"), 512.0, 256.0, A.mult, A.add, ["x"], ["k4"])
-    ts(fc("k5"), fc("x"), -512.0, -256.0, A.mult, A.add, ["x"], ["k5"])
-    for n in ("WZP", "WZN", "WZZ", "WZF", "WZC", "WZM"): fill(Wt(n), 0, ["z" + n])
+        act(fc(n), oh(k), F.Identity, scale=c, bias=oh(prev) if isinstance(prev, int) else fc(prev))
+    col("u1", A3, 16.0, WR); col("f1", RS, -128.0, "u1"); col("f2", ONE, -39.0, "f1"); col("f5", L5, 1.0, L6)
+    col("fa", RS, -1.0, A3)
+    ts(fc("k1"), fc("x"), float(WR), 4096.0, A.is_ge, A.mult); ts(fc("hi"), fc("k1"), 1.0, None, A.max)
+    col("fb", PR, -2.0, "fa"); col("fn", A4, 1.0, NR)
+    ts(fc("fp"), oh(15), 256.0, 1.0, A.mult, A.add)
+    ts(fc("xm"), fc("x"), -15.0, 1.0 / 2048, A.add, A.mult)
+    ts(fc("thr"), fc("x"), -1.0, 15.75, A.mult, A.add)
+    ts(fc("sb"), fc("x"), 512.0, -8064.0, A.mult, A.add)
+    fill(fc("k2"), -2048); fill(fc("k3"), 16); fill(fc("k4"), -16)
 
-    def wcol(n, r, c):
-        s, tk = (c, []) if isinstance(c, float) else ((oh(c), ["oh"]) if isinstance(c, int) else (fc(c), [c]))
-        act(Wc(n, r), Wc("BLK", 0), F.Identity, ["BLK", "z" + n] + tk, [n + str(r)], scale=s)
-    zc = [("WZZ", 0, 0), ("WZZ", 1, "f1"), ("WZZ", 2, "f2"), ("WZZ", 3, "u4"), ("WZZ", 5, "f5"),
-          ("WZF", 1, "xm"), ("WZF", 2, "xn"), ("WZF", 5, -4096.0), ("WZC", 6, 1.0), ("WZP", 3, "fp"), ("WZN", 3, 1.0),
-          ("WZM", 3, 1.0), ("WZM", 4, 1.0)]
-    for n, r, c in zc: wcol(n, r, c)
-    zt_ = lambda n: [a + str(r) for a, r, c in zc if a == n]
-    act(Wt("WZS"), Wt("BLK"), F.Identity, ["BLK", "f23"], ["WZS"], scale=fc("f23"))
-    act(Wt("WZP2"), Wt("WZS"), F.Identity, ["WZS"], ["WZP2"], scale=-0.5)
-    act(Wt("WZN2"), Wt("BLK"), F.Identity, ["BLK", "f40"], ["WZN2"], scale=fc("f40"))
-    act(Wc("WZN2", 0), Wc("BLK", 0), F.Identity, ["BLK", "oh"], ["WZN2"], scale=oh(4))
-    act(Wt("WL"), Wt("BLK"), F.Identity, ["BLK", "f5"], ["WL"], scale=fc("f5"))
-    act(Wt("WLX"), Wt("WL"), F.Identity, ["WL"], ["WLX"], scale=-2048.0)
-    act(Wt("WW"), Wt("BLK"), F.Identity, ["BLK", "oh"], ["WW"], scale=oh(1))
-    ts(T.mc[:], T.jr[:], fc("x"), -8192.0, A.not_equal, A.mult, ["jr", "x"], ["mc"])
-    tt(T.mx[:], T.dg[:], T.mc[:], A.add, ["dg", "mc"], ["mx"])
-    ts(T.tf[:], T.top[:], 1152.0, None, A.add, None, ["top"], ["tf"])
-    fill(T.pb[:, 2048:2064], 0, ["pbx"]); fill(T.tc[:, 2048:2056], -1, ["tcx"]); fill(T.zt[:, 2048:2064], 0, ["ztx"])
-    fill(fc("k0"), -128, ["k0"]); fill(fc("k1"), -17 * 4096, ["k1"]); fill(fc("k2"), -2048, ["k2"]); fill(fc("k3"), 16, ["k3"])
-    lo = lambda b: L * b if b < NB - 1 else L * b - L
-    fills = [[[] for _ in range(NS)] for _ in range(NB)]
-    for b in range(NB):
-        edges = [768]
-        for t in range(NS - 1): edges += [768 + 192 * t + lo(b), 768 + 192 * t + lo(b) + 2 * L]
-        for j in range(0, len(edges) - 1, 2):
-            if edges[j + 1] > edges[j]:
-                for t in range(j // 2 + 1, NS): fills[b][t].append("mz%d_%d" % (b, j))
-                fill(T["mm%d" % b][:, edges[j]:edges[j + 1]], 0, ["mz%d_%d" % (b, j)])
+    def whole(n, y, c): ts(Wt(n), Wt("YB"), float(y), c, A.is_equal, A.mult)
+    def more(n, y, c, k=None, s=16):
+        if k is None: act(Wc(n, y, s), Wc("BLK", y, s), F.Identity, scale=c)
+        else: ts(Wc(n, y, s), Wc("BLK", y, s), c, k, A.mult, A.mult)
+    whole("WZZ", ONE, oh(ONE)); more("WZZ", A3, oh(ONE), -271.0); more("WZZ", A4, oh(ONE)); more("WZZ", L5, fc("f5"))
+    more("WZZ", WR, fc("f1")); more("WZZ", RS, fc("f2"))
+    whole("WZF", L5, -1.0); more("WZF", RS, fc("xm"), None, WR - RS)
+    whole("WZC", L6, 1.0); whole("WZP", A3, fc("fp")); more("WZP", PR, 1.0)
+    whole("WZG", A3, 1.0); more("WZG", A4, oh(0), -256.0); more("WZG", NR, 1.0)
+    whole("WZM", A3, oh(0)); more("WZM", A4, oh(0))
+    ts(Wt("WZA"), Wt("BLK"), fc("fa"), -0.5, A.mult, A.mult)
+    ts(Wt("WZ2"), Wt("BLK"), fc("fb"), -0.5, A.mult, A.mult)
+    act(Wt("WZB"), Wt("BLK"), F.Identity, scale=fc("fn"))
+    iota(v("rs"), [[0, 12], [4096, 16]], 0)
+    iota(v("r0"), [[-16, 12], [8192, 16]], 2048)
+    iota(v("top"), [[1, 192]], 576)
+    iota(v("dg"), [[1, 192]], 1850)
+    ts(v("mc"), v("jr"), fc("x"), -8192.0, A.not_equal, A.mult)
+    ts(v("r2"), v("r0"), fc("x"), None, A.subtract)
+    fill(v("pb", 2048, 2240), -1); fill(v("zt", 2048, 2240), 0)
+    for c in range(2): fill(v("clb", 1280 + 388 * c, 1668 + 388 * c), -1)
+    iota(v("tf"), [[1, 192]], 1728)
+    band("LE", "BLK", [[-1, 128]], 1, 0, A.is_ge, 0.0)
 
-    tb = [7, 6, 7, 6]
-    for c in range(4):
-        sl = slice(512 * c, 512 * c + 512); tk = "pt%d" % (c // 2)
-        ts(T.fl[:, sl], T.ptb[:, sl], 255.0, None, A.is_equal, None, [tk], ["fl%d" % c], 0.5)
-        mm(tb[c], T["ps%d" % tb[c]][:], [(Wt("I0"), T.ptb[:, sl], ["I0", tk], 1), (Wt("I40"), T.fl[:, sl], ["I40", "fl%d" % c], 1)])
-        if c % 2: cp(T.gt[:, sl], T["ps%d" % tb[c]][:], [], ["gt%d" % c], banks=[tb[c]])
-        else: act(T.gt[:, sl], T["ps%d" % tb[c]][:], F.Identity, [], ["gt%d" % c], banks=[tb[c]])
-    GT = ["gt%d" % c for c in range(4)]
-    cp(T.af[0:8, 0:192], T.ai[0:8, 0:192], ["ai0"], ["af0"])
-    cp(T.af[0:8, 192:768], T.ai[0:8, 192:768], ["ai1", "ai2", "ai3"], ["af1"])
-    tt(T.qa[:], T.top[:], T.qi[:], A.subtract, ["top", "qi"], ["qa"])
+    swap = {(0, 0): v("ie", 16, 144), (0, 1): v("ie", 0, 128), (1, 1): v("iod", 16, 144), (1, 0): v("iod", 32, 160)}
     for h in range(2):
-        sl = slice(128 * h, 128 * h + 128); kb = bk("sc", NB - 1); pb_ = T["ps%d" % kb][:, 128 * h:128 + 128 * h]
-        cp(T.xf[:, sl], T.xb[:, sl], ["xb%d" % (8 * h + k) for k in range(8)], ["xf%d" % h])
-        mm(kb, pb_, [(T.xf[:, sl], T.i32[:], ["xf%d" % h, "i32"], 4)])
-        ts(T.bw[:, sl], pb_, -1.0, None, A.mult, None, [], ["bw%d" % h], banks=[kb])
+        x0 = 128 * h
+        cp(v("xh", x0, x0 + 128), v("xb", x0, x0 + 128))
+        add("V", lambda x0=x0: g.vector.transpose(T.xt[:, x0:x0 + 128], T.xh[:, x0:x0 + 128]), [v("xh", x0, x0 + 128)],
+            [v("xt", x0, x0 + 128)], COST["v0"] + 64 * cy)
+        for c in range(8):
+            mm(v("ps%d" % (5 - 2 * h), c, 128, 8),
+               [(swap[(c % 2, k)], v("xt", x0 + 32 * (c // 2) + 16 * k, x0 + 32 * (c // 2) + 16 * k + 16)) for k in range(2)])
+        cp(v("bw", x0, x0 + 128), v("ps%d" % (5 - 2 * h), 0, 128))
     for c in range(4):
-        sl = slice(512 * c, 512 * c + 512)
-        act(T.pb[:, sl], T.ptb[:].indirect(T.bw[:, 32 * c:32 * c + 32]), F.Identity, ["pt0", "pt1", "bw0"], ["pb%d" % c], gather=True)
-        ts(T.zt[:, sl], T.pb[:, sl], 255.0, 256.0, A.not_equal, A.mult, ["pb%d" % c], ["zt%d" % c], 0.5)
-        ts(T.tc[:, sl], T.clb[:].indirect(T.bw[:, 128 + 32 * c:160 + 32 * c]), 1.0 / 4096, None, A.mult, None, ["cl", "bw1"], ["tc%d" % c], gather=True)
-    PB = ["pb%d" % c for c in range(4)] + ["pbx"]
-    ZT = ["zt%d" % c for c in range(4)] + ["ztx"]
-    TC = ["tc%d" % c for c in range(4)] + ["tcx"]
+        sl = (512 * c, 512 * c + 512); pk = v("ps%d" % (7 - c % 2))
+        ts(v("fl", *sl), v("ptb", *sl), 255.0, BIG, A.is_equal, A.mult)
+        mm(pk, [(Wt("I0"), v("ptb", *sl)), (Wt("I0"), v("fl", *sl))])
+        move("V" if c % 2 else "S", v("gt", *sl), pk)
+    cp(v("af", 0, 192, 1, top8), v("ai", 0, 192, 1, top8))
+    ts(v("af", 192, 384, 1, top8), v("ai", 192, 384, 1, top8), -1.0, 16.0, A.mult, A.add)
+    cp(v("af", 384, 768, 1, top8), v("ai", 384, 768, 1, top8))
+    for c in range(4):
+        sl = (512 * c, 512 * c + 512)
+        move("S", v("pb", *sl), ind(v("ptb"), v("bw", 32 * c, 32 * c + 32)))
+        ts(v("zt", *sl), v("pb", *sl), 255.0, 256.0, A.not_equal, A.mult)
+        move(ON["tc"], v("tc", *sl), ind(v("clb", 0, 1280), v("bw", 128 + 32 * c, 160 + 32 * c)))
 
-    def wrap(b, reg, buf, idx, s1, s2, op0, op1):
-        sb = str(b); o = T[buf + sb]
-        add("V", lambda: g.vector.tensor_tensor_scan(o[:], T.rs[:, 0:L], ps(reg, b), 0.0, A.min, A.max),
-            ["rs"], [buf + sb], vcost(L, 1.0), [bk(reg, b)])
-        ts(T[idx + sb][:, 0:W], o[:, 15:L:16], s1, s2, op0, op1, [buf + sb], [idx + sb])
+    a_ = lambda j, a=0, b=192: v("af", 192 * j + a, 192 * j + b, 1, top8)
+    mm(v("ps1", 0, 192), [(Wt("I0"), v("mc")), (Wt("RR", top8), a_(0))])
+    scan(v("s1"), v("rs"), v("ps1", 0, 192), 0.0)
+    cp(v("i0", 0, 12), v("s1", 15, 192, 16))
+    mm(v("ps0", 0, 384), [(Wt("RR", top8), v("af", 384, 768, 1, top8))])
+    ts(v("f0"), v("ps0", 0, 192), fc("x"), None, A.is_gt)
+    ts(v("zp"), v("ps0", 192, 384), oh(WR), oh(ONE), A.mult, A.add)
+    tt(v("qa"), v("qi"), v("top"), A.subtract)
+    tt(v("e0"), v("qa"), v("f0"), A.mult)
+    tt(v("mx"), v("dg"), v("mc"), A.add)
 
-    past = [[(Wt("WDT"), T.e0[:, L * b:L * b + L], ["WDT", "e0%d" % b], 1)] for b in range(NB)]
+    def wrap(b, reg, reset, init, buf, idx, s1, s2, op0, op1=None):
+        scan(v(buf), reset, ps(reg, b), init)
+        ts(v(idx, 0, W), v(buf, 15, L, 16), s1, s2, op0, op1)
+
+    def steps01(b, s):
+        out = v("pg%d" % b, 2 * L * s, 2 * L * (s + 1))
+        if ON["pg"] == "S": act(out, ps("P", b, 2), F.Sigmoid, bias=fc("sb"), scale=512.0)
+        else: ts(out, ps("P", b, 2), fc("thr"), None, A.is_ge)
+
+    past = [[(Wt("WDT"), v("e0", L * b, L * b + L))] for b in range(NB)]
+
+    def clauses(b, win, idx):
+        cu, keep, cf = v("cu%d" % b), v("tc", 2048 + L * b, 2048 + L * b + L), v("cf%d" % b)
+        cp(cu, ind(win, idx))
+        cp(keep, cu)
+        if ON["cf"] != "G": move(ON["cf"], cf, keep if ON["cf"] == "S" else cu)
+        else: add("G", lambda: g.affine_select(cf[0], keep[0], [[0, L]], A.is_ge, 0.0, 0, 0), [keep], [cf], 170.0 + 2 * L * cy)
 
     def look(b, s):
-        sb = str(b); c0 = L * b
-        tt(T["pd" + sb][:], T["pf" + sb][:, 2 * L * s:2 * L * s + L], DQ(b), A.mult, ["P%s_%d" % (sb, s)], ["pd" + sb], [bk("dq", b)])
+        sb = str(b)
+        tt(v("pd" + sb), v("pg" + sb, 2 * L * s, 2 * L * s + L), ps("dq", b), A.mult)
         if s - 1 in KEEP:
-            act(T["dq" + sb][:], DQ(b), F.Identity, [], ["dq" + sb], banks=[bk("dq", b)])
-            past[b][:] = [(Wt("I0"), T["dq" + sb][:], ["I0", "dq" + sb], 1)]
-        pm("xr", b, [(Wt("I0"), T.mx[:, c0:c0 + L], ["I0", "mx"], 1), (Wt("BLK"), T["pd" + sb][:], ["BLK", "pd" + sb], 1)])
-        wrap(b, "xr", "sx", "iy", 192.0 * s - 1024.0, None, A.add, None)
+            move(ON["dq"], v("dq" + sb), ps("dq", b))
+            past[b][:] = [(Wt("I0"), v("dq" + sb))]
+        mm(ps("xr", b), [(Wt("I0"), v("mx", L * b, L * b + L)), (Wt("BLK"), v("pd" + sb))])
+        wrap(b, "xr", v("rs", 0, L), 0.0, "sx" + sb, "iy" + sb, 576.0 + 192 * s - 1850, None, A.add)
 
     def zlayer(b, out, terms):
-        pm("z", b, terms)
-        ts(T[out + str(b)][:], ps("z", b), 0.0, fc("hi"), A.max, A.min, ["hi"], [out + str(b)], banks=[bk("z", b)])
-
-    once = [1300.0]
-
-    def step01(out, name, b, n, w):
-        if ON_S["pf"]:
-            act(out, ps(name, b, n), F.Sigmoid, ["k0"], w, bias=fc("k0"), scale=512.0, banks=[bk(name, b)], extra=once[0]); once[0] = 0.0
-        else: ts(out, ps(name, b, n), 0.5, None, A.is_ge, None, [], w, banks=[bk(name, b)])
+        mm(ps("z", b), terms)
+        ts(out, ps("z", b), 0.0, fc("hi"), A.max, A.min)
 
     for b in range(NB):
         sb = str(b); c0 = L * b; cur[0] = b
-        a_ = lambda j: T.af[0:8, 192 * j + c0:192 * j + c0 + L]
-        pm("cr", b, [(Wt("I0"), T.mc[:, 0:L], ["I0", "mc"], 1), (Wt("RR", 8), a_(0), ["RR", "af0"], 1)])
-        wrap(b, "cr", "sc", "ix", 0.0, None, A.add, None)
-        cp(T["cu" + sb][:], T.clb[:].indirect(T["ix" + sb][:, 0:W]), ["cl", "ix" + sb], ["cu" + sb], gather=True)
-        ts(T["cf" + sb][:], T["cu" + sb][:], 1.0 / 4096, None, A.mult, None, ["cu" + sb], ["cf" + sb], 0.5)
-        for j, nm in enumerate(("P", "F", "fd")): pm(nm, b, [(Wt("RR", 8), a_(1 + j), ["RR", "af1"], 1)])
-        act(T["pf" + sb][:, 0:L], ps("P", b), F.Sigmoid, ["k4"], ["P%s_0" % sb], bias=fc("k4"), scale=-512.0, banks=[bk("P", b)], extra=once[0])
-        once[0] = 0.0
-        act(T["pf" + sb][:, L:2 * L], ps("F", b), F.Sigmoid, ["k5"], ["F%s_0" % sb], bias=fc("k5"), scale=512.0, banks=[bk("F", b)])
-        ts(T["zp" + sb][:], ps("fd", b), fc("c1"), fc("c2"), A.mult, A.add, ["c1", "c2"], ["zp" + sb], banks=[bk("fd", b)])
-        tt(T.e0[:, c0:c0 + L], T.qa[:, c0:c0 + L], T["pf" + sb][:, L:2 * L], A.mult, ["qa", "F%s_0" % sb], ["e0" + sb])
-        pm("dq", b, past[b])
+        clauses(b, v("clb", 0, 1280), v("i0", W * b, W * b + W))
+        for j, nm in enumerate("PG"): mm(ps(nm, b), [(Wt("RR", top8), a_(1 + j, c0, c0 + L))])
+        steps01(b, 0)
+        mm(ps("dq", b), past[b])
         look(b, 0)
-        zlayer(b, "zz", [(Wt("I0"), T["zp" + sb][:], ["I0", "zp" + sb], 1), (Wt("WZP"), T["pf" + sb][:, 0:L], zt_("WZP") + ["P%s_0" % sb], 1),
-                         (Wt("WZN"), T["pf" + sb][:, L:2 * L], zt_("WZN") + ["F%s_0" % sb], 1)])
+        zlayer(b, v("zz" + sb), [(Wt("WZZ"), v("zp", c0, c0 + L)), (Wt("WZM"), v("pb", 2048, 2048 + L)),
+                                 (Wt("WZP"), v("pg" + sb, 0, L)), (Wt("WZG"), v("pg" + sb, L, 2 * L))])
+    cur[0] = 0
+    dma("Y", v("clb", 0, 2048, 1, row0), T.gs[:], 65536, False)
+    act(Wt("WL"), Wt("BLK"), F.Identity, scale=fc("f5"))
+    ts(Wt("WLX"), Wt("BLK"), fc("f5"), -2048.0, A.mult, A.mult)
+    act(Wt("WW"), Wt("BLK"), F.Identity, scale=oh(WR))
+    ts(Wt("X0"), Wt("BLK"), oh(0), 1.0 / 256, A.mult, A.mult)
 
-    LC = L // GC
     KS = 16 // R
     for t in range(NS):
         for b in range(NB):
             sb = str(b); c0 = L * b; end = t == NS - 1; cur[0] = b
-            B = lambda n: T[n + sb]
-            f0 = 2 * L * t; P_, F_, Z_ = B("pf")[:, f0:f0 + L], B("pf")[:, f0 + L:f0 + 2 * L], B("zz")[:]
-            pt_, ft_ = "P%s_%d" % (sb, t), "F%s_%d" % (sb, t)
-            gtok = ["gg%s_%d" % (sb, c) for c in range(GC)]
-            for c in range(GC):
-                act(B("gg")[:, 16 * LC * c:16 * LC * (c + 1)], T.gt[:].indirect(B("cu")[:, LC * c:LC * c + LC]), F.Identity,
-                    GT + ["cu" + sb], [gtok[c]], gather=True)
-            we = 768 if t == 0 else 768 + 192 * (t - 1) + c0 + L
-            act(B("mv")[:], B("mm")[:, 0:we].indirect(B("iy")[:, 0:W]), F.Identity,
-                ["m0_" + sb, "iy" + sb] + fills[b][t] + ["M%s_%d" % (sb, u) for u in range(t)], ["mv" + sb], gather=True)
-            mp = T["ps%d" % bk("m", b)]
-            for j in range(R): mm(bk("m", b), mp[:, j:R * L:R], [(Wt("I0"), B("mv")[:], ["I0", "mv" + sb], 1)])
-            pm("sc", b, [(T.b2[:, 15 - k:143 - k], B("gg")[:, k:16 * L:16], ["b2"] + gtok, 1) for k in range(16)], last=False)
-            pm("sc", b, [(Wt("WZS"), Z_, ["WZS", "zz" + sb], 1)], first=False, last=False)
-            for j in range(KS):
-                tt(B("ee")[:, j:16 * L:KS], B("gg")[:, j:16 * L:KS], mp[:, 0:R * L], A.is_equal, gtok, ["ee%s_%d" % (sb, j)], [bk("m", b)])
-            pm("sc", b, [(T.b1[:, 15 - k:143 - k], B("ee")[:, k:16 * L:16], ["b1", "ee%s_%d" % (sb, k % KS)], 1)
-                         for k in sorted(range(16), key=lambda k: k % KS)], first=False)
-            act(B("ok")[:], ps("sc", b), F.Relu, ["k1"], ["ok" + sb], bias=fc("k1"), scale=4096.0, banks=[bk("sc", b)])
-            o0 = 2 * L * (NB * t + b); om, of = (o0, o0 + L) if b < NB - 1 else (o0 + L, o0)
-            fi = T.outb[:, of:of + L]; ft = "fi%s_%d" % (sb, t)
-            pm("u", b, [(Wt("N4K"), B("cf")[:], ["N4K", "cf" + sb], 1), (Wt("TRI"), B("ok")[:], ["TRI", "ok" + sb], 1)])
-            if ON_S["cs"]: act(B("cs")[:], ps("u", b), F.Relu, ["k2"], ["cs" + sb], bias=fc("k2"), banks=[bk("u", b)])
-            else: ts(B("cs")[:], ps("u", b), -2048.0, 0.0, A.add, A.max, [], ["cs" + sb], banks=[bk("u", b)])
-            pm("cr", b, [(Wt("I0"), T.mc[:, 0:L], ["I0", "mc"], 1), (Wt("BLK"), B("cs")[:], ["BLK", "cs" + sb], 1)])
-            if ON_S["fi"]: act(fi, B("cs")[:], F.Sign, ["cs" + sb], [ft])
-            else: ts(fi, B("cs")[:], 1.0, None, A.min, None, ["cs" + sb], [ft], 0.5)
-            wrap(b, "cr", "sc", "ix", -1.0, 2048.0, A.mult, A.add)
-            ix = B("ix")[:, 0:W]; oc = slice(192 * t + c0, 192 * t + c0 + L); otk = "o%s_%d" % (sb, t); mtk = "M%s_%d" % (sb, t)
-            tt(B("bt")[:], T.zt[:].indirect(ix), B("mv")[:], A.max, ZT + ["ix" + sb, "mv" + sb], ["bt" + sb], gather=True)
-            tt(T.outb[:, om:om + L], T.pb[:].indirect(ix), B("bt")[:], A.min, PB + ["ix" + sb, "bt" + sb], [otk], gather=True)
-            l0 = 768 + 192 * t + lo(b)
-            land = B("mm")[:, l0 + of - o0:l0 + of - o0 + L]
-            fn, cnt = send(t, B("mm")[:, l0:l0 + 2 * L], T.outb[:, o0:o0 + 2 * L], "a%d_%d" % (b, t))
-            add("G", fn, [otk, ft], [mtk], 300.0, lat=COST["rem"] + (COST["rem0"] if t + b == 0 else 0.0), sem=("a%d_%d" % (b, t), cnt))
-            dma("Y", T.mn[:, oc], B("mm")[:, 768 + 192 * t + c0:768 + 192 * t + c0 + L], [mtk], [], 256 * L, False)
-            pm("fd", b, [(Wt("BLK"), fi, ["BLK", ft], 1)])
-            pm("P", b, [(Wt("WPP"), P_, ["WPP", pt_], 1), (Wt("WZP2"), Z_, ["WZP2", "zz" + sb], 1), (Wt("WFP"), fi, ["WFP", ft], 1)])
-            pm("F", b, [(Wt("WNN"), F_, ["WNN", ft_], 1), (Wt("WZN2"), Z_, ["WZN2", "zz" + sb], 1), (Wt("WFN"), fi, ["WFN", ft], 1)])
-            if not end:
-                tt(B("xx")[:], B("cf")[:], ps("fd", b), A.subtract, ["cf" + sb], ["xx" + sb], [bk("fd", b)])
-                tt(B("cf")[:], T.tc[:].indirect(ix), B("xx")[:], A.max, TC + ["ix" + sb, "xx" + sb], ["cf" + sb], gather=True)
-                ts(B("cu")[:], B("cf")[:], 4096.0, None, A.mult, None, ["cf" + sb], ["cu" + sb], 0.5)
-            t1 = B("t1")[:, L * t:L * t + L]; tk = "t1%s_%d" % (sb, t)
-            tt(t1, B("pd")[:], ps("fd", b), A.mult, ["pd" + sb], [tk], [bk("fd", b)])
-            f0 += 2 * L; P_, F_ = B("pf")[:, f0:f0 + L], B("pf")[:, f0 + L:f0 + 2 * L]
-            pt_, ft_ = "P%s_%d" % (sb, t + 1), "F%s_%d" % (sb, t + 1)
-            step01(B("pf")[:, f0:f0 + 2 * L], "P", b, 2, [pt_, ft_])
-            past[b] += [(Wt("WDT"), t1, ["WDT", tk], 1), (Wt("WDN"), F_, ["WDN", ft_], 1)]
-            pm("dq", b, past[b])
-            zt0 = [(Wt("WZZ"), Z_, zt_("WZZ") + ["zz" + sb], 1), (Wt("WZF"), fi, zt_("WZF") + [ft], 1),
-                   (Wt("WZC"), B("cs")[:], zt_("WZC") + ["cs" + sb], 1)]
-            zt1 = [(Wt("WZP"), P_, zt_("WZP") + [pt_], 1), (Wt("WZN"), F_, zt_("WZN") + [ft_], 1)]
-            zt2 = [(Wt("WZM"), land, zt_("WZM") + [mtk], 1)]
+            B = lambda n, *a: v(n + sb, *a)
+            Z = B("zz")
+            for q, l0, l1 in PIECES: move(q, B("gg", 16 * l0, 16 * l1), ind(v("gt"), B("cu", l0, l1)))
+            move(ON["mv"], B("mv"), ind(v("mm", 0, 768 if t == 0 else 576 + 192 * t + c0 + L), B("iy", 0, W)))
+            for j in range(R): mm(v("ps%d" % (2 * b), j, R * L, R), [(Wt("I0"), B("mv"))])
+            mm(ps("sc", b), [(v("b2", 16 - k, 144 - k), B("gg", k, 16 * L, 16)) for k in range(16)] + [(Wt("WZA"), Z)], last=False)
+            for j in range(KS): tt(B("ee", j, 16 * L, KS), B("gg", j, 16 * L, KS), ps("m", b, R), A.is_equal)
+            mm(ps("u", b), [(Wt("NI"), B("cf"))], last=False)
+            mm(ps("sc", b), [(v("b1", 16 - k, 144 - k), B("ee", k, 16 * L, 16)) for k in sorted(range(16), key=lambda k: k % KS)], first=False)
+            if ON["ok"] == "S": act(B("ok"), ps("sc", b), F.Relu, bias=fc("k4"), scale=-2.0)
+            else: ts(B("ok"), ps("sc", b), -8.25, None, A.is_le)
+            mm(ps("cr", b), [(Wt("I0"), v("mc", 0, L))], last=False)
+            mm(ps("u", b), [(Wt("TRI"), B("ok"))], first=False)
+            mm(ps("fi", b), [(Wt("TRI"), B("ok"))])
+            if ON["cs"] == "S": act(B("cs"), ps("u", b, 2), F.Relu, bias=fc("k2"))
+            else: ts(B("cs"), ps("u", b, 2), -2048.0, 0.0, A.add, A.max)
+            cs, fi = B("cs", 0, L), B("cs", L, 2 * L)
+            mm(ps("cr", b), [(Wt("BLK"), cs), (Wt("BLK"), fi)], first=False)
+            wrap(b, "cr", v("r2", c0, c0 + L), 8192.0, "sc" + sb, "ix" + sb, -1.0, 4096.0, A.mult, A.add)
+            ix = B("ix", 0, W); o0 = 192 * t + c0
+            src = [v("outa", o0, o0 + L), v("outb", o0, o0 + L)]
+            tt(src[0], ind(v("zt"), ix), B("mv"), A.max)
+            if ON["fold"]: move(ON["pb"], src[1], ind(v("pb"), ix))
+            else: tt(src[1], ind(v("pb"), ix), src[0], A.min); src = src[1:]
+            land = v("mm", 768 + o0, 768 + o0 + L)
+            fn, cnt = send(t, land[0], [x[0] for x in src], "a%d_%d" % (b, t))
+            add("G", fn, src, [land], 300.0, COST["rem"] + (COST["rem0"] if t + b == 0 else 0.0), ("a%d_%d" % (b, t), cnt))
+            if not end: clauses(b, v("tc", 0, 2048 + c0 + L), ix)
+            mm(ps("fd", b), [(Wt("NBD"), fi)])
+            mm(ps("P", b), [(Wt("WZ2"), Z), (Wt("BLK"), fi)])
+            mm(ps("G", b), [(Wt("WZB"), Z), (Wt("NBD"), fi)])
+            t1 = B("t1", L * t, L * t + L)
+            tt(t1, B("pd"), ps("fd", b), A.mult)
+            steps01(b, t + 1)
+            P_, G_ = B("pg", 2 * L * (t + 1), 2 * L * (t + 1) + L), B("pg", 2 * L * (t + 1) + L, 2 * L * (t + 2))
+            past[b] += [(Wt("WDT"), t1), (Wt("WDN"), G_)]
+            mm(ps("dq", b), past[b])
+            zt0 = [(Wt("WZZ"), Z), (Wt("WZF"), fi), (Wt("WZC"), cs)]
+            if b == NB - 1 or end:
+                a0 = o0 if end else 192 * t
+                if ON["mn"] == "S": act(v("mo", a0, o0 + L), v("mm", 768 + a0, 768 + o0 + L), F.Relu)
+                else: ts(v("mo", a0, o0 + L), v("mm", 768 + a0, 768 + o0 + L), 0.0, None, A.max)
+                dma("Y", T.mn[:, a0:o0 + L], v("mo", a0, o0 + L), 256 * (o0 + L - a0), False)
             if not end:
                 look(b, t + 1)
-                zlayer(b, "zz", zt0 + zt1 + zt2)
+                zlayer(b, Z, zt0 + [(Wt("WZP"), P_), (Wt("WZG"), G_), (Wt("WZM"), land)])
                 continue
-            cp(B("pd")[:], DQ(b), [], ["pd" + sb], banks=[bk("dq", b)])
-            zlayer(b, "zp", zt0)
-            pm("m", b, [(Wt("I0"), T.tf[:, c0:c0 + L], ["I0", "tf"], 1), (Wt("LE"), B("pd")[:], ["LE", "pd" + sb], 1)])
-            pm("cr", b, [(Wt("I0"), T.mc[:, 0:L], ["I0", "mc"], 1), (Wt("WL"), B("zp")[:], ["WL", "zp" + sb], 1)])
-            wrap(b, "cr", "sx", "iy", -1.0, 2048.0, A.mult, A.add)
-            pm("sc", b, [(Wt("RR", 8), T.af[0:8, c0:c0 + L], ["RR", "af0"], 1), (Wt("WLX"), B("zp")[:], ["WLX", "zp" + sb], 1)])
-            pm("fi", b, [(Wt("BLK"), P_, ["BLK", pt_], 1)])
-            pm("xr", b, [(Wt("WW"), B("zp")[:], ["WW", "zp" + sb], 1)])
-            act(B("xx")[:], ps("sc", b), F.Identity, [], ["xx" + sb], banks=[bk("sc", b)])
-            act(T.ysb[:, 192 + c0:192 + c0 + L], ps("fi", b), F.Identity, ["k3"], ["yp" + sb], bias=fc("k3"), scale=-1.0, banks=[bk("fi", b)])
-            act(T.ysb[:, 576 + c0:576 + c0 + L], ps("xr", b), F.Identity, [], ["yw" + sb], banks=[bk("xr", b)])
-            tt(T.ysb[:, c0:c0 + L], T.gst[:].indirect(B("iy")[:, 0:W]), B("xx")[:], A.max,
-               ["gs%d" % c for c in range(4)] + ["iy" + sb, "xx" + sb], ["ys" + sb], gather=True)
-            pm("F", b, [(Wt("WNN"), F_, ["WNN", ft_], 1), (Wt("WZN2"), B("zp")[:], ["WZN2", "zp" + sb], 1), (Wt("BLK"), land, ["BLK", mtk], 1)])
-            ts(B("f2")[:], ps("F", b), 0.5, None, A.is_ge, None, [], ["f2" + sb], banks=[bk("F", b)])
-            tt(T.yqb[:, c0:c0 + L], B("f2")[:], ps("m", b), A.mult, ["f2" + sb], ["yq" + sb], [bk("m", b)])
-            dma("Y", T.yq[:, c0:c0 + L], T.yqb[:, c0:c0 + L], ["yq" + sb], [], 512 * L, False)
-            pm("yn", b, [(Wt("BLK"), F_, ["BLK", ft_], 1), (Wt("BLK"), land, ["BLK", mtk], 1)])
-            ts(T.ysb[:, 384 + c0:384 + c0 + L], ps("yn", b), 16.0, None, A.min, None, [], ["yn" + sb], banks=[bk("yn", b)])
-    dma("S", T.ys[:], T.ysb[0:128:16, :], [n + str(b) for n in ("ys", "yp", "yn", "yw") for b in range(NB)], [], 24576, False)
+            zp = v("zp", c0, c0 + L)
+            move("S", B("pd"), ps("dq", b))
+            zlayer(b, zp, zt0)
+            mm(ps("m", b), [(Wt("I0"), v("tf", c0, c0 + L)), (Wt("LE"), B("pd"))])
+            mm(ps("cr", b), [(Wt("I0"), v("mc", 0, L)), (Wt("WL"), zp)])
+            wrap(b, "cr", v("rs", 0, L), 0.0, "sx" + sb, "iy" + sb, -1.0, 2048.0, A.mult, A.add)
+            mm(ps("y1", b), [(Wt("RR", top8), a_(0, c0, c0 + L)), (Wt("WLX"), zp)])
+            mm(ps("y2", b), [(Wt("BLK"), P_)])
+            mm(ps("y3", b), [(Wt("WW"), zp)])
+            act(B("xx"), ps("y1", b), F.Identity)
+            act(v("ysb", 192 + c0, 192 + c0 + L), ps("y2", b), F.Identity, bias=fc("k3"), scale=-1.0)
+            act(v("ysb", 576 + c0, 576 + c0 + L), ps("y3", b), F.Identity)
+            tt(v("ysb", c0, c0 + L), ind(v("clb"), B("iy", 0, W)), B("xx"), A.max)
+            mm(ps("sc", b), [(Wt("BLK"), G_), (Wt("X0"), land)])
+            ts(B("f2"), ps("sc", b), fc("x"), None, A.is_ge)
+            tt(v("yqb", c0, c0 + L), B("f2"), ps("m", b), A.mult)
+            dma("Y", T.yq[:, c0:c0 + L], v("yqb", c0, c0 + L), 512 * L, False)
+            mm(ps("fd", b), [(Wt("BLK"), B("f2"))])
+            act(v("ysb", 384 + c0, 384 + c0 + L), ps("fd", b), F.Identity)
+    dma("S", T.ys[:], v("ysb", 0, 768, 1, row0), 24576, False)
     return ops
 
 
-GUESSES = [(1.0, 110.0, 70.0, 1.0, 0.0), (1.7, 110.0, 70.0, 1.0, 0.0), (1.0, 220.0, 140.0, 1.0, 0.0), (1.0, 110.0, 70.0, 1.4, 0.0),
-           (1.0, 60.0, 40.0, 0.7, 0.0), (1.0, 110.0, 70.0, 1.0, 50.0)]
+GUESSES = [(0.9, 0.92, 130.0, 130.0, 1.0), (1.1, 1.1, 130.0, 130.0, 1.0), (1.3, 1.35, 130.0, 130.0, 1.0), (1.0, 1.0, 190.0, 190.0, 1.0),
+           (1.0, 1.0, 130.0, 130.0, 1.3), (1.1, 1.1, 80.0, 80.0, 0.8)]
 ORDER = {}
 
 
@@ -443,7 +449,7 @@ def schedule(ops):
 
     def length(seq):
         total = 0.0
-        for pe, hop, own, rem, extra in GUESSES:
+        for pe, vs, hop, own, rem in GUESSES:
             free, fin = {}, [0.0] * n
             for i in seq:
                 o = ops[i]; e = o["e"]; s = free.get(e, 0.0)
@@ -451,7 +457,7 @@ def schedule(ops):
                     ej = ops[j]["e"]
                     r = fin[j] + ops[j]["lat"] * (rem if ej == "G" else 1.0) + (own if ej == e else hop)
                     if r > s: s = r
-                fin[i] = free[e] = s + cost[i] * (pe if e == "P" else 1.0) + (extra if e in "VS" else 0.0)
+                fin[i] = free[e] = s + cost[i] * (pe if e == "P" else vs if e in "VS" else 1.0)
             total += max(fin[i] + ops[i]["lat"] for i in range(n))
         return total
     zero = [0.0] * n
@@ -479,7 +485,7 @@ def schedule(ops):
             key = [-back[i] + noise[i] for i in range(n)]
             for i in range(n):
                 for j, gap in pre[i]: key[i] = max(key[i], key[j] + 1e-3)
-    ORDER[n] = (best[1], best[2])
+    ORDER[n] = best[1]
     return ORDER[n]
 
 
@@ -503,23 +509,34 @@ def rank_program(g, core, T, topo):
         rid, pid = topo.addr(dst, core)
         m = common(core)
         total[0] += bin(m).count("1")
-        return (lambda: g.remote_dma(land, src, T.sem[sem], T.sem.sent, pid, rid, m)), bin(common(cores[(rank - d) % n])).count("1")
+        if len(src) == 1:
+            return (lambda: g.remote_dma(land, src[0], T.sem[sem], T.sem.sent, pid, rid, m)), bin(common(cores[(rank - d) % n])).count("1")
+        fold = RemoteDMATransfer(dst_ids=[DstId(rid=rid, pnc=pid)], dma_engine_mask=m, remote_sem=T.sem[sem], srcs=src, dsts=[land], alu_op=3)
+        return (lambda: g.remote_dma_fused([fold], local_sem=T.sem.sent)), bin(common(cores[(rank - d) % n])).count("1")
 
     ops = build(g, T, send)
-    seq, fin = schedule(ops)
+    seq = schedule(ops)
+    place = {i: k for k, i in enumerate(seq)}
+    known, after, waits = {}, {}, {}
+    for i in seq:
+        o = ops[i]; kn = known.setdefault(o["e"], {}); mine = []
+        for j in sorted(o["dep"], key=lambda j: -place[j]):
+            key = ops[j]["sem"][0] if ops[j]["sem"] else ops[j]["e"]
+            if kn.get(key, -1) >= place[j]: continue
+            mine.append(j)
+            for k, x in after[j].items():
+                if kn.get(k, -1) < x: kn[k] = x
+        waits[i] = mine
+        after[i] = dict(kn); after[i][o["sem"][0] if o["sem"] else o["e"]] = place[i]
     need = set()
-    for o in ops: need.update(o["dep"])
+    for w in waits.values(): need.update(w)
     queue = {"V": g.vector, "S": g.scalar, "P": g.tensor, "G": g, "Y": g.sync}
-    count, mark, seen, waited = {}, {}, {}, {}
+    count, mark, waited = {}, {}, {}
     for i in seq:
         o = ops[i]; q = queue[o["e"]]
-        want = {}
-        for j in o["dep"]:
-            s, v = mark[j]
-            want[s] = max(want.get(s, 0), v)
-        for s, v in want.items():
-            if seen.get((o["e"], s), 0) < v:
-                q.wait_ge(T.sem[s], v); seen[(o["e"], s)] = v; waited[s] = max(waited.get(s, 0), v)
+        for j in waits[i]:
+            s, x = mark[j]
+            q.wait_ge(T.sem[s], x); waited[s] = max(waited.get(s, 0), x)
         ins = o["fn"]()
         if o["sem"]:
             mark[i] = o["sem"]; count[o["sem"][0]] = o["sem"][1]
@@ -528,5 +545,5 @@ def rank_program(g, core, T, topo):
             s = "c" + o["e"]; count[s] = count.get(s, 0) + 1; mark[i] = (s, count[s])
             ins.then_inc(T.sem[s], 1)
     g.wait_ge(T.sem.sent, total[0])
-    for s, v in count.items():
-        if waited.get(s, 0) < v: g.sync.wait_ge(T.sem[s], v)
+    for s, x in count.items():
+        if waited.get(s, 0) < x: g.sync.wait_ge(T.sem[s], x)

import numpy as np
from concourse.bass import DstId, RemoteDMATransfer
from concourse.mybir import AluOpType as A, ActivationFunctionType as F

NB = 3
L = 192 // NB
W = L // 16
R = 4
PIECES = [("S", 0, L // 2), ("S", L // 2, L)]
KEEP = (1, 3)
ON = {"ok": "V", "cs": "S", "pg": "S", "mv": "S", "dq": "S", "mn": "V", "tc": "V", "pb": "S", "cf": "G", "fold": False}
H16 = "float16"
NS = 6
BIG = float(2 ** 40)
ONE, RS, A3, A4, WR, L5, L6, PR, NR = 0, 1, 3, 4, 9, 10, 11, 12, 13
WN = ["BLK", "I0", "NI", "DD", "SS", "LE", "TRI", "WDT", "WDN", "NBD", "RR", "WZA", "WZ2", "WZB", "WZZ", "WZF", "WZC", "WZP", "WZG", "WZM",
      "WL", "WLX", "WW", "X0", "YB"]

SCRATCH = {
    "ptb": ("sbuf", [128, 2048], "bfloat16"), "fl": ("sbuf", [128, 2048], "bfloat16"), "gt": ("sbuf", [128, 2048], "bfloat16"),
    "clb": ("sbuf", [128, 2056], "int32"), "xb": ("sbuf", [128, 256], "int32"), "xh": ("sbuf", [128, 256], H16),
    "xt": ("sbuf", [128, 256], H16), "bw": ("sbuf", [128, 256], "uint16"),
    "pb": ("sbuf", [128, 2240], "bfloat16"), "zt": ("sbuf", [128, 2240], "bfloat16"), "tc": ("sbuf", [128, 2240], "float32"),
    "mm": ("sbuf", [128, 1920], "bfloat16"), "mo": ("sbuf", [128, 1152], "bfloat16"), "outb": ("sbuf", [128, 1152], "bfloat16"),
    "outa": ("sbuf", [128, 1152], "bfloat16"),
    "ai": ("sbuf", [128, 768], "int32"), "af": ("sbuf", [128, 768], H16), "qi": ("sbuf", [128, 192], "int32"),
    "qa": ("sbuf", [128, 192], H16), "top": ("sbuf", [128, 192], "float32"), "f0": ("sbuf", [128, 192], H16),
    "jr": ("sbuf", [128, 192], "bfloat16"), "jb": ("sbuf", [128, 128], "bfloat16"), "j1": ("sbuf", [128, 128], "bfloat16"),
    "jf": ("sbuf", [128, 160], "bfloat16"), "ic": ("sbuf", [128, 8], "int32"),
    "fc": ("sbuf", [128, 40], "float32"), "oh": ("sbuf", [128, 16], "float32"),
    "b1": ("sbuf", [128, 160], "bfloat16"), "b2": ("sbuf", [128, 160], "bfloat16"),
    "ie": ("sbuf", [128, 160], H16), "iod": ("sbuf", [128, 160], H16),
    "wt": ("sbuf", [128, 128 * len(WN)], H16),
    "mc": ("sbuf", [128, 192], H16), "mx": ("sbuf", [128, 192], H16), "dg": ("sbuf", [128, 192], H16),
    "rs": ("sbuf", [128, 192], "float32"), "r0": ("sbuf", [128, 192], "float32"), "r2": ("sbuf", [128, 192], "float32"),
    "tf": ("sbuf", [128, 192], H16), "e0": ("sbuf", [128, 192], H16), "s1": ("sbuf", [128, 192], "float32"),
    "i0": ("sbuf", [128, 16], "uint16"), "zp": ("sbuf", [128, 192], H16),
    "yqb": ("sbuf", [128, 192], "float32"), "ysb": ("sbuf", [128, 768], "float32"),
}
for _b in range(NB):
    for _n, _s, _d in (("gg", 16 * L, "bfloat16"), ("ee", 16 * L, "bfloat16"), ("cu", L, "uint16"), ("xx", L, "float32"),
                       ("ok", L, H16), ("cs", 2 * L, H16), ("sc", L, "float32"), ("sx", L, "float32"), ("ix", 16, "uint16"),
                       ("iy", 16, "uint16"), ("mv", L, "bfloat16"), ("bt", L, "bfloat16"), ("pg", 14 * L, H16),
                       ("t1", 6 * L, H16), ("pd", L, H16), ("cf", L, H16), ("dq", L, H16), ("zz", L, H16), ("f2", L, H16)):
        SCRATCH[_n + str(_b)] = ("sbuf", [128, _s], _d)
for _b in range(8):
    SCRATCH["ps" + str(_b)] = ("psum", [128, 512], "float32")

SEMAPHORES = (["cV", "cS", "cP", "cG", "sent"] + ["d%d" % _i for _i in range(40)]
              + ["a%d_%d" % (_b, _t) for _b in range(NB) for _t in range(NS)])

COST = {"cy": 0.9, "v0": 20.0, "s0": 75.0, "g": 1.6, "pe": 0.58, "hop": 130.0, "self": 130.0, "rem": 2500.0, "rem0": 2800.0,
        "dma": 1500.0, "bw": 200.0, "skews": [1200.0, 2000.0, 2800.0], "rounds": 150, "noise": 150.0, "seed": 1}

PLACE = {"m": (0, 0), "u": (0, 4), "fi": (0, 5), "P": (0, 6), "G": (0, 7), "dq": (0, 4), "xr": (0, 5),
         "sc": (1, 0), "cr": (1, 1), "fd": (1, 2), "y1": (1, 3), "y2": (1, 4), "y3": (1, 5), "z": (6, 0)}


def build(g, T, send):
    ops, wr, rd, bank, cur = [], {}, {}, {}, [0]
    cy = COST["cy"]

    def v(name, a=0, b=None, s=1, p=None):
        t = T[name]
        if b is None: b = t.shape[1]
        m = 0
        if s == 1: m = ((1 << (b - a)) - 1) << a
        else:
            for c in range(a, b, s): m |= 1 << c
        return (t[p if p else slice(0, 128), slice(a, b, s) if s > 1 else slice(a, b)], [(name, m)])

    def ind(win, off): return (win[0].indirect(off[0]), win[1] + off[1])
    ap = lambda x: x[0] if isinstance(x, tuple) else x

    def add(eng, fn, ins, outs, cost, lat=0.0, sem=None, chain=None):
        i = len(ops)
        dep, order = set(), set()
        reads = [k for x in ins if isinstance(x, tuple) for k in x[1]]
        writes = [k for x in outs for k in x[1]]
        banks = set(n for n, m in reads + writes if n[:2] == "ps")
        if chain: banks.add(chain)
        for b in banks:
            last = bank.setdefault(b, {})
            for e, j in last.items():
                if e != eng: dep.add(j)
                else: order.add(j)
            last[eng] = i
        for n, m in reads:
            if n in banks: continue
            dep.update(j for k, j in wr.get(n, ()) if k & m)
        for n, m in writes:
            if n in banks: continue
            dep.update(j for k, j in wr.get(n, ()) if k & m)
            dep.update(j for k, j in rd.get(n, ()) if k & m)
            wr[n] = [(k & ~m, j) for k, j in wr.get(n, ()) if k & ~m] + [(m, i)]
            rd[n] = [(k & ~m, j) for k, j in rd.get(n, ()) if k & ~m]
        for n, m in reads:
            if n not in banks: rd.setdefault(n, []).append((m, i))
        dep.discard(i)
        ops.append({"e": eng, "fn": fn, "dep": dep, "ord": order, "c": cost, "lat": lat, "sem": sem, "b": cur[0]})

    n_of = lambda x: x[0].shape[1]
    gath = lambda x: len(x[1]) > 1
    two = lambda *xs: all(SCRATCH[x[1][0][0]][2] in ("bfloat16", H16, "uint16") for x in xs)
    psum = lambda x: x[1][0][0][:2] == "ps"

    def vcost(out, in0, f):
        if gath(in0): return 60.0 + n_of(out) * COST["g"] * cy
        return COST["v0"] + max(64.0, n_of(out) * f) * cy

    def ts(out, in0, s1, s2, op0, op1=None):
        if op1 is None: fn = lambda: g.vector.tensor_scalar(out[0], in0[0], ap(s1), None, op0)
        else: fn = lambda: g.vector.tensor_scalar(out[0], in0[0], ap(s1), ap(s2), op0, op1)
        add("V", fn, [in0, s1, s2], [out], vcost(out, in0, 0.5 if two(out, in0) else 1.0))

    def tt(out, in0, in1, op):
        add("V", lambda: g.vector.tensor_tensor(out[0], in0[0], in1[0], op), [in0, in1], [out],
            vcost(out, in0, 1.0 if psum(in0) or psum(in1) else 2.0))

    def cp(out, in_):
        add("V", lambda: g.vector.tensor_copy(out[0], in_[0]), [in_], [out], vcost(out, in_, 0.5 if two(out, in_) else 1.0))

    def scan(out, d0, d1, init):
        add("V", lambda: g.vector.tensor_tensor_scan(out[0], d0[0], d1[0], init, A.min, A.max), [d0, d1], [out], vcost(out, d0, 1.0))

    once = [1300.0]

    def act(out, in_, func, bias=0.0, scale=1.0):
        c = COST["s0"] + n_of(out) * cy * (COST["g"] if gath(in_) else 1.0)
        if func == F.Sigmoid: c += once[0]; once[0] = 0.0
        add("S", lambda: g.scalar.activation(out[0], in_[0], func, bias=ap(bias), scale=ap(scale)), [in_, bias, scale], [out], c)

    def move(q, out, in_):
        if q == "S": act(out, in_, F.Identity)
        else: cp(out, in_)

    def mm(out, terms, first=True, last=True):
        for j, term in enumerate(terms):
            lh, rh = term[:2]; o = term[2] if len(term) > 2 else out
            st, sp = first and j == 0, last and j == len(terms) - 1
            add("P", lambda o=o, lh=lh, rh=rh, st=st, sp=sp: g.tensor.matmul(o[0], lh[0], rh[0], st, sp), [lh, rh], [o],
                max(64.0, n_of(rh)) * COST["pe"] * (1 if two(rh) else 4))

    def iota(out, pat, base, mul=0):
        if SCRATCH[out[1][0][0]][2] == "int32": fn = lambda: g.iota(out[0], pat, base, mul)
        else: fn = lambda: g.iota(out[0], pat, base, mul, allow_small_or_imprecise_dtypes=True)
        add("G", fn, [], [out], 130.0 + 2 * n_of(out) * cy)

    def fill(out, val): iota(out, [[0, n_of(out)]], val)

    def band(n, src, pat, mul, base, op, other):
        add("G", lambda: g.affine_select(Wt(n)[0], Wt(src)[0], pat, op, other, base, mul), [Wt(src)], [Wt(n)], 170.0 + 256 * cy)

    nd, queued = [0], [0.0]

    def dma(q, out, in_, nbytes, load=True):
        s = "d%d" % nd[0]; nd[0] += 1
        eng = g.sync if q == "Y" else g.scalar
        if load: queued[0] += nbytes / COST["bw"]
        lat = COST["dma"] + (queued[0] if load else nbytes / COST["bw"])
        add(q, lambda: eng.dma_start(ap(out), ap(in_)), [in_], [out] if isinstance(out, tuple) else [], 60.0, lat, (s, 16),
            "load" if load else None)

    def Wt(n, p=None): return v("wt", 128 * WN.index(n), 128 * WN.index(n) + 128, 1, p)
    def Wc(n, r, s=16): return v("wt", 128 * WN.index(n) + r, 128 * WN.index(n) + 128, s)

    def ps(name, b, n=1):
        k, a = PLACE[name]
        if k == 6: k, a = 6 + b % 2, b
        else: k += 2 * b
        return v("ps%d" % k, a * L, (a + n) * L)

    top8 = slice(0, 8)
    row0 = slice(0, 128, 16)

    dma("Y", v("xb", 0, 128), T.bo[:], 65536)
    for j, n in enumerate(("s0", "p0", "n0", "w0")):
        dma("Y", v("ai", 192 * j, 192 * j + 192, 1, top8), T[n][:], 6144)
    for c in range(2): dma("Y", v("ptb", 1024 * c, 1024 * c + 1024), T.pt[:, 1024 * c:1024 * c + 1024], 262144)
    dma("Y", v("clb", 0, 1280), T.cl[:], 655360)
    dma("Y", v("qi"), T.q0[:], 98304)
    dma("Y", v("mm", 0, 768), T.m0[:], 196608)
    dma("Y", v("xb", 128, 256), T.gs[:], 65536)

    names = ["g16", "x", "h", "p", "p16", "g32", "a32", "s32", "pe", "po", "u0", "f1", "f2", "f5", "u1", "hi", "fp", "xm", "fa", "fb", "fn",
             "thr", "sb", "k1", "k2", "k3", "k4"]
    fc = lambda n: v("fc", names.index(n), names.index(n) + 1)
    oh = lambda k: v("oh", k, k + 1)
    iota(v("ic", 0, 1), [[1, 1]], 0, 1)
    iota(fc("p"), [[1, 1]], 0, 1)
    iota(v("jf"), [[1, 160]], -16)
    iota(v("jb"), [[16, 8], [0, 16]], 0)
    iota(v("j1"), [[32, 8], [1, 16]], 0)
    iota(v("jr"), [[0, 12], [1, 16]], 0)
    iota(fc("p16"), [[1, 1]], 0, 16)
    for j, bits in enumerate((112, 15, 16)): ts(v("ic", 1 + j, 2 + j), v("ic", 0, 1), bits, None, A.bitwise_and)
    cp(v("fc", 0, 3), v("ic", 1, 4))
    ts(fc("pe"), fc("h"), 64.0, fc("p"), A.mult, A.add)
    ts(fc("u0"), fc("h"), -64.0, 1024.0, A.mult, A.add)
    ts(fc("po"), fc("u0"), fc("p"), None, A.add)
    ts(v("ie"), v("jf"), fc("pe"), None, A.is_equal)
    ts(v("iod"), v("jf"), fc("po"), None, A.is_equal)
    ts(Wt("BLK"), v("jb"), fc("g16"), None, A.is_equal)
    ts(Wt("RR", top8), v("jb", 0, 128, 1, top8), v("fc", names.index("p16"), names.index("p16") + 1, 1, top8), None, A.is_equal)
    ts(v("b1"), v("jf"), fc("g16"), -0.5, A.is_equal, A.mult)
    ts(v("b2"), v("jf"), fc("g16"), -0.5 / BIG, A.is_equal, A.mult)
    act(fc("g32"), fc("g16"), F.Identity, scale=2.0)
    act(fc("a32"), fc("g16"), F.Identity, bias=fc("p"))
    act(fc("s32"), fc("x"), F.Identity, scale=-1.0, bias=fc("g32"))
    ts(Wt("DD"), v("j1"), fc("a32"), None, A.subtract)
    ts(Wt("SS"), v("j1"), fc("s32"), None, A.subtract)
    ts(Wt("YB"), v("j1"), fc("g32"), None, A.subtract)
    ts(Wt("I0"), Wt("DD"), 0.0, None, A.is_equal)
    act(Wt("NI"), Wt("I0"), F.Identity, scale=-1.0)
    diag = ([[1, 128]], -1, 0)
    ts(Wt("WDT"), Wt("DD"), -1.0, -1.0, A.is_equal, A.mult); band("WDT", "WDT", *diag, A.not_equal, 1.0)
    ts(Wt("WDN"), Wt("SS"), 14.0, 192.0, A.is_equal, A.mult); band("WDN", "WDN", [[-16, 8], [1, 16]], 1, -15, A.not_equal, -192.0)
    act(Wt("TRI"), Wt("BLK"), F.Identity, scale=-4096.0)
    band("TRI", "TRI", *diag, A.is_gt, 0.0); band("TRI", "TRI", *diag, A.not_equal, 4096.0)
    act(Wt("NBD"), Wt("BLK"), F.Identity, scale=-1.0 / 2048)
    ts(v("oh"), v("jr", 0, 16), fc("x"), None, A.is_equal)

    def col(n, k, c, prev):
        act(fc(n), oh(k), F.Identity, scale=c, bias=oh(prev) if isinstance(prev, int) else fc(prev))
    col("u1", A3, 16.0, WR); col("f1", RS, -128.0, "u1"); col("f2", ONE, -39.0, "f1"); col("f5", L5, 1.0, L6)
    col("fa", RS, -1.0, A3)
    ts(fc("k1"), fc("x"), float(WR), 4096.0, A.is_ge, A.mult); ts(fc("hi"), fc("k1"), 1.0, None, A.max)
    col("fb", PR, -2.0, "fa"); col("fn", A4, 1.0, NR)
    ts(fc("fp"), oh(15), 256.0, 1.0, A.mult, A.add)
    ts(fc("xm"), fc("x"), -15.0, 1.0 / 2048, A.add, A.mult)
    ts(fc("thr"), fc("x"), -1.0, 15.75, A.mult, A.add)
    ts(fc("sb"), fc("x"), 512.0, -8064.0, A.mult, A.add)
    fill(fc("k2"), -2048); fill(fc("k3"), 16); fill(fc("k4"), -16)

    def whole(n, y, c): ts(Wt(n), Wt("YB"), float(y), c, A.is_equal, A.mult)
    def more(n, y, c, k=None, s=16):
        if k is None: act(Wc(n, y, s), Wc("BLK", y, s), F.Identity, scale=c)
        else: ts(Wc(n, y, s), Wc("BLK", y, s), c, k, A.mult, A.mult)
    whole("WZZ", ONE, oh(ONE)); more("WZZ", A3, oh(ONE), -271.0); more("WZZ", A4, oh(ONE)); more("WZZ", L5, fc("f5"))
    more("WZZ", WR, fc("f1")); more("WZZ", RS, fc("f2"))
    whole("WZF", L5, -1.0); more("WZF", RS, fc("xm"), None, WR - RS)
    whole("WZC", L6, 1.0); whole("WZP", A3, fc("fp")); more("WZP", PR, 1.0)
    whole("WZG", A3, 1.0); more("WZG", A4, oh(0), -256.0); more("WZG", NR, 1.0)
    whole("WZM", A3, oh(0)); more("WZM", A4, oh(0))
    ts(Wt("WZA"), Wt("BLK"), fc("fa"), -0.5, A.mult, A.mult)
    ts(Wt("WZ2"), Wt("BLK"), fc("fb"), -0.5, A.mult, A.mult)
    act(Wt("WZB"), Wt("BLK"), F.Identity, scale=fc("fn"))
    iota(v("rs"), [[0, 12], [4096, 16]], 0)
    iota(v("r0"), [[-16, 12], [8192, 16]], 2048)
    iota(v("top"), [[1, 192]], 576)
    iota(v("dg"), [[1, 192]], 1850)
    ts(v("mc"), v("jr"), fc("x"), -8192.0, A.not_equal, A.mult)
    ts(v("r2"), v("r0"), fc("x"), None, A.subtract)
    fill(v("pb", 2048, 2240), -1); fill(v("zt", 2048, 2240), 0)
    for c in range(2): fill(v("clb", 1280 + 388 * c, 1668 + 388 * c), -1)
    iota(v("tf"), [[1, 192]], 1728)
    band("LE", "BLK", [[-1, 128]], 1, 0, A.is_ge, 0.0)

    swap = {(0, 0): v("ie", 16, 144), (0, 1): v("ie", 0, 128), (1, 1): v("iod", 16, 144), (1, 0): v("iod", 32, 160)}
    for h in range(2):
        x0 = 128 * h
        cp(v("xh", x0, x0 + 128), v("xb", x0, x0 + 128))
        add("V", lambda x0=x0: g.vector.transpose(T.xt[:, x0:x0 + 128], T.xh[:, x0:x0 + 128]), [v("xh", x0, x0 + 128)],
            [v("xt", x0, x0 + 128)], COST["v0"] + 64 * cy)
        for c in range(8):
            mm(v("ps%d" % (5 - 2 * h), c, 128, 8),
               [(swap[(c % 2, k)], v("xt", x0 + 32 * (c // 2) + 16 * k, x0 + 32 * (c // 2) + 16 * k + 16)) for k in range(2)])
        cp(v("bw", x0, x0 + 128), v("ps%d" % (5 - 2 * h), 0, 128))
    for c in range(4):
        sl = (512 * c, 512 * c + 512); pk = v("ps%d" % (7 - c % 2))
        ts(v("fl", *sl), v("ptb", *sl), 255.0, BIG, A.is_equal, A.mult)
        mm(pk, [(Wt("I0"), v("ptb", *sl)), (Wt("I0"), v("fl", *sl))])
        move("V" if c % 2 else "S", v("gt", *sl), pk)
    cp(v("af", 0, 192, 1, top8), v("ai", 0, 192, 1, top8))
    ts(v("af", 192, 384, 1, top8), v("ai", 192, 384, 1, top8), -1.0, 16.0, A.mult, A.add)
    cp(v("af", 384, 768, 1, top8), v("ai", 384, 768, 1, top8))
    for c in range(4):
        sl = (512 * c, 512 * c + 512)
        move("S", v("pb", *sl), ind(v("ptb"), v("bw", 32 * c, 32 * c + 32)))
        ts(v("zt", *sl), v("pb", *sl), 255.0, 256.0, A.not_equal, A.mult)
        move(ON["tc"], v("tc", *sl), ind(v("clb", 0, 1280), v("bw", 128 + 32 * c, 160 + 32 * c)))

    a_ = lambda j, a=0, b=192: v("af", 192 * j + a, 192 * j + b, 1, top8)
    mm(v("ps1", 0, 192), [(Wt("I0"), v("mc")), (Wt("RR", top8), a_(0))])
    scan(v("s1"), v("rs"), v("ps1", 0, 192), 0.0)
    cp(v("i0", 0, 12), v("s1", 15, 192, 16))
    mm(v("ps0", 0, 384), [(Wt("RR", top8), v("af", 384, 768, 1, top8))])
    ts(v("f0"), v("ps0", 0, 192), fc("x"), None, A.is_gt)
    ts(v("zp"), v("ps0", 192, 384), oh(WR), oh(ONE), A.mult, A.add)
    tt(v("qa"), v("qi"), v("top"), A.subtract)
    tt(v("e0"), v("qa"), v("f0"), A.mult)
    tt(v("mx"), v("dg"), v("mc"), A.add)

    def wrap(b, reg, reset, init, buf, idx, s1, s2, op0, op1=None):
        scan(v(buf), reset, ps(reg, b), init)
        ts(v(idx, 0, W), v(buf, 15, L, 16), s1, s2, op0, op1)

    def steps01(b, s):
        out = v("pg%d" % b, 2 * L * s, 2 * L * (s + 1))
        if ON["pg"] == "S": act(out, ps("P", b, 2), F.Sigmoid, bias=fc("sb"), scale=512.0)
        else: ts(out, ps("P", b, 2), fc("thr"), None, A.is_ge)

    past = [[(Wt("WDT"), v("e0", L * b, L * b + L))] for b in range(NB)]

    def clauses(b, win, idx):
        cu, keep, cf = v("cu%d" % b), v("tc", 2048 + L * b, 2048 + L * b + L), v("cf%d" % b)
        cp(cu, ind(win, idx))
        cp(keep, cu)
        if ON["cf"] != "G": move(ON["cf"], cf, keep if ON["cf"] == "S" else cu)
        else: add("G", lambda: g.affine_select(cf[0], keep[0], [[0, L]], A.is_ge, 0.0, 0, 0), [keep], [cf], 170.0 + 2 * L * cy)

    def look(b, s):
        sb = str(b)
        tt(v("pd" + sb), v("pg" + sb, 2 * L * s, 2 * L * s + L), ps("dq", b), A.mult)
        if s - 1 in KEEP:
            move(ON["dq"], v("dq" + sb), ps("dq", b))
            past[b][:] = [(Wt("I0"), v("dq" + sb))]
        mm(ps("xr", b), [(Wt("I0"), v("mx", L * b, L * b + L)), (Wt("BLK"), v("pd" + sb))])
        wrap(b, "xr", v("rs", 0, L), 0.0, "sx" + sb, "iy" + sb, 576.0 + 192 * s - 1850, None, A.add)

    def zlayer(b, out, terms):
        mm(ps("z", b), terms)
        ts(out, ps("z", b), 0.0, fc("hi"), A.max, A.min)

    for b in range(NB):
        sb = str(b); c0 = L * b; cur[0] = b
        clauses(b, v("clb", 0, 1280), v("i0", W * b, W * b + W))
        for j, nm in enumerate("PG"): mm(ps(nm, b), [(Wt("RR", top8), a_(1 + j, c0, c0 + L))])
        steps01(b, 0)
        mm(ps("dq", b), past[b])
        look(b, 0)
        zlayer(b, v("zz" + sb), [(Wt("WZZ"), v("zp", c0, c0 + L)), (Wt("WZM"), v("pb", 2048, 2048 + L)),
                                 (Wt("WZP"), v("pg" + sb, 0, L)), (Wt("WZG"), v("pg" + sb, L, 2 * L))])
    cur[0] = 0
    dma("Y", v("clb", 0, 2048, 1, row0), T.gs[:], 65536, False)
    act(Wt("WL"), Wt("BLK"), F.Identity, scale=fc("f5"))
    ts(Wt("WLX"), Wt("BLK"), fc("f5"), -2048.0, A.mult, A.mult)
    act(Wt("WW"), Wt("BLK"), F.Identity, scale=oh(WR))
    ts(Wt("X0"), Wt("BLK"), oh(0), 1.0 / 256, A.mult, A.mult)

    KS = 16 // R
    for t in range(NS):
        for b in range(NB):
            sb = str(b); c0 = L * b; end = t == NS - 1; cur[0] = b
            B = lambda n, *a: v(n + sb, *a)
            Z = B("zz")
            for q, l0, l1 in PIECES: move(q, B("gg", 16 * l0, 16 * l1), ind(v("gt"), B("cu", l0, l1)))
            move(ON["mv"], B("mv"), ind(v("mm", 0, 768 if t == 0 else 576 + 192 * t + c0 + L), B("iy", 0, W)))
            for j in range(R): mm(v("ps%d" % (2 * b), j, R * L, R), [(Wt("I0"), B("mv"))])
            mm(ps("sc", b), [(v("b2", 16 - k, 144 - k), B("gg", k, 16 * L, 16)) for k in range(16)] + [(Wt("WZA"), Z)], last=False)
            for j in range(KS): tt(B("ee", j, 16 * L, KS), B("gg", j, 16 * L, KS), ps("m", b, R), A.is_equal)
            mm(ps("u", b), [(Wt("NI"), B("cf"))], last=False)
            mm(ps("sc", b), [(v("b1", 16 - k, 144 - k), B("ee", k, 16 * L, 16)) for k in sorted(range(16), key=lambda k: k % KS)], first=False)
            if ON["ok"] == "S": act(B("ok"), ps("sc", b), F.Relu, bias=fc("k4"), scale=-2.0)
            else: ts(B("ok"), ps("sc", b), -8.25, None, A.is_le)
            mm(ps("cr", b), [(Wt("I0"), v("mc", 0, L))], last=False)
            mm(ps("u", b), [(Wt("TRI"), B("ok"))], first=False)
            mm(ps("fi", b), [(Wt("TRI"), B("ok"))])
            if ON["cs"] == "S": act(B("cs"), ps("u", b, 2), F.Relu, bias=fc("k2"))
            else: ts(B("cs"), ps("u", b, 2), -2048.0, 0.0, A.add, A.max)
            cs, fi = B("cs", 0, L), B("cs", L, 2 * L)
            mm(ps("cr", b), [(Wt("BLK"), cs), (Wt("BLK"), fi)], first=False)
            wrap(b, "cr", v("r2", c0, c0 + L), 8192.0, "sc" + sb, "ix" + sb, -1.0, 4096.0, A.mult, A.add)
            ix = B("ix", 0, W); o0 = 192 * t + c0
            src = [v("outa", o0, o0 + L), v("outb", o0, o0 + L)]
            tt(src[0], ind(v("zt"), ix), B("mv"), A.max)
            if ON["fold"]: move(ON["pb"], src[1], ind(v("pb"), ix))
            else: tt(src[1], ind(v("pb"), ix), src[0], A.min); src = src[1:]
            land = v("mm", 768 + o0, 768 + o0 + L)
            fn, cnt = send(t, land[0], [x[0] for x in src], "a%d_%d" % (b, t))
            add("G", fn, src, [land], 300.0, COST["rem"] + (COST["rem0"] if t + b == 0 else 0.0), ("a%d_%d" % (b, t), cnt))
            if not end: clauses(b, v("tc", 0, 2048 + c0 + L), ix)
            mm(ps("fd", b), [(Wt("NBD"), fi)])
            mm(ps("P", b), [(Wt("WZ2"), Z), (Wt("BLK"), fi)])
            mm(ps("G", b), [(Wt("WZB"), Z), (Wt("NBD"), fi)])
            t1 = B("t1", L * t, L * t + L)
            tt(t1, B("pd"), ps("fd", b), A.mult)
            steps01(b, t + 1)
            P_, G_ = B("pg", 2 * L * (t + 1), 2 * L * (t + 1) + L), B("pg", 2 * L * (t + 1) + L, 2 * L * (t + 2))
            past[b] += [(Wt("WDT"), t1), (Wt("WDN"), G_)]
            mm(ps("dq", b), past[b])
            zt0 = [(Wt("WZZ"), Z), (Wt("WZF"), fi), (Wt("WZC"), cs)]
            if b == NB - 1 or end:
                a0 = o0 if end else 192 * t
                if ON["mn"] == "S": act(v("mo", a0, o0 + L), v("mm", 768 + a0, 768 + o0 + L), F.Relu)
                else: ts(v("mo", a0, o0 + L), v("mm", 768 + a0, 768 + o0 + L), 0.0, None, A.max)
                dma("Y", T.mn[:, a0:o0 + L], v("mo", a0, o0 + L), 256 * (o0 + L - a0), False)
            if not end:
                look(b, t + 1)
                zlayer(b, Z, zt0 + [(Wt("WZP"), P_), (Wt("WZG"), G_), (Wt("WZM"), land)])
                continue
            zp = v("zp", c0, c0 + L)
            move("S", B("pd"), ps("dq", b))
            zlayer(b, zp, zt0)
            mm(ps("m", b), [(Wt("I0"), v("tf", c0, c0 + L)), (Wt("LE"), B("pd"))])
            mm(ps("cr", b), [(Wt("I0"), v("mc", 0, L)), (Wt("WL"), zp)])
            wrap(b, "cr", v("rs", 0, L), 0.0, "sx" + sb, "iy" + sb, -1.0, 2048.0, A.mult, A.add)
            mm(ps("y1", b), [(Wt("RR", top8), a_(0, c0, c0 + L)), (Wt("WLX"), zp)])
            mm(ps("y2", b), [(Wt("BLK"), P_)])
            mm(ps("y3", b), [(Wt("WW"), zp)])
            act(B("xx"), ps("y1", b), F.Identity)
            act(v("ysb", 192 + c0, 192 + c0 + L), ps("y2", b), F.Identity, bias=fc("k3"), scale=-1.0)
            act(v("ysb", 576 + c0, 576 + c0 + L), ps("y3", b), F.Identity)
            tt(v("ysb", c0, c0 + L), ind(v("clb"), B("iy", 0, W)), B("xx"), A.max)
            mm(ps("sc", b), [(Wt("BLK"), G_), (Wt("X0"), land)])
            ts(B("f2"), ps("sc", b), fc("x"), None, A.is_ge)
            tt(v("yqb", c0, c0 + L), B("f2"), ps("m", b), A.mult)
            dma("Y", T.yq[:, c0:c0 + L], v("yqb", c0, c0 + L), 512 * L, False)
            mm(ps("fd", b), [(Wt("BLK"), B("f2"))])
            act(v("ysb", 384 + c0, 384 + c0 + L), ps("fd", b), F.Identity)
    dma("S", T.ys[:], v("ysb", 0, 768, 1, row0), 24576, False)
    return ops


GUESSES = [(0.9, 0.92, 130.0, 130.0, 1.0), (1.1, 1.1, 130.0, 130.0, 1.0), (1.3, 1.35, 130.0, 130.0, 1.0), (1.0, 1.0, 190.0, 190.0, 1.0),
           (1.0, 1.0, 130.0, 130.0, 1.3), (1.1, 1.1, 80.0, 80.0, 0.8)]
ORDER = {}


def schedule(ops):
    n = len(ops)
    if n in ORDER: return ORDER[n]
    pre = [[] for _ in range(n)]
    suc = [[] for _ in range(n)]
    for i, o in enumerate(ops):
        for j in o["dep"] | o["ord"]:
            gap = 0.0
            if j in o["dep"]: gap = ops[j]["lat"] + (COST["self"] if ops[j]["e"] == o["e"] else COST["hop"])
            pre[i].append((j, gap)); suc[j].append((i, gap))
    cost = [o["c"] for o in ops]

    def sweep(order, before, head):
        busy, fin = {}, [0.0] * n
        for i in order:
            s = head[i]
            for j, gap in before[i]:
                if fin[j] + gap > s: s = fin[j] + gap
            a, b = busy.setdefault(ops[i]["e"], ([], []))
            lo, hi = 0, len(b)
            while lo < hi:
                mid = (lo + hi) // 2
                if b[mid] > s: hi = mid
                else: lo = mid + 1
            k = lo
            while k < len(a) and a[k] < s + cost[i]:
                s = max(s, b[k]); k += 1
            a.insert(k, s); b.insert(k, s + cost[i]); fin[i] = s + cost[i]
        return fin

    def length(seq):
        total = 0.0
        for pe, vs, hop, own, rem in GUESSES:
            free, fin = {}, [0.0] * n
            for i in seq:
                o = ops[i]; e = o["e"]; s = free.get(e, 0.0)
                for j in o["dep"]:
                    ej = ops[j]["e"]
                    r = fin[j] + ops[j]["lat"] * (rem if ej == "G" else 1.0) + (own if ej == e else hop)
                    if r > s: s = r
                fin[i] = free[e] = s + cost[i] * (pe if e == "P" else vs if e in "VS" else 1.0)
            total += max(fin[i] + ops[i]["lat"] for i in range(n))
        return total
    zero = [0.0] * n
    tail = [o["lat"] for o in ops]
    best = None
    rnd = np.random.RandomState(COST["seed"])
    for skew in COST["skews"]:
        prio = [0.0] * n
        for i in range(n - 1, -1, -1):
            prio[i] = cost[i] + max([tail[i]] + [gap + prio[k] for k, gap in suc[i]])
        key = [-(prio[i] - skew * ops[i]["b"]) for i in range(n)]
        for i in range(n):
            for j, gap in pre[i]: key[i] = max(key[i], key[j] + 1e-3)
        for it in range(COST["rounds"]):
            fin = sweep(sorted(range(n), key=lambda i: key[i]), pre, zero)
            seq = sorted(range(n), key=lambda i: (fin[i] - cost[i], i))
            end = length(seq)
            if best is None or end < best[0]: best = (end, seq, fin)
            noise = rnd.rand(n) * COST["noise"]
            key = [-fin[i] + noise[i] for i in range(n)]
            for i in range(n - 1, -1, -1):
                for k, gap in suc[i]: key[i] = max(key[i], key[k] + 1e-3)
            back = sweep(sorted(range(n), key=lambda i: key[i]), suc, tail)
            noise = rnd.rand(n) * COST["noise"]
            key = [-back[i] + noise[i] for i in range(n)]
            for i in range(n):
                for j, gap in pre[i]: key[i] = max(key[i], key[j] + 1e-3)
    ORDER[n] = best[1]
    return ORDER[n]


def rank_program(g, core, T, topo):
    rank = T.rank_of(core)
    if rank is None:
        return
    cores = T.cores
    n = len(cores)

    def common(c):
        m = -1
        for d in cores:
            if d != c: m &= topo.mask(c, d)
        return m
    total = [0]

    def send(t, land, src, sem):
        d = 1 + t % (n - 1)
        dst = cores[(rank + d) % n]
        rid, pid = topo.addr(dst, core)
        m = common(core)
        total[0] += bin(m).count("1")
        if len(src) == 1:
            return (lambda: g.remote_dma(land, src[0], T.sem[sem], T.sem.sent, pid, rid, m)), bin(common(cores[(rank - d) % n])).count("1")
        fold = RemoteDMATransfer(dst_ids=[DstId(rid=rid, pnc=pid)], dma_engine_mask=m, remote_sem=T.sem[sem], srcs=src, dsts=[land], alu_op=3)
        return (lambda: g.remote_dma_fused([fold], local_sem=T.sem.sent)), bin(common(cores[(rank - d) % n])).count("1")

    ops = build(g, T, send)
    seq = schedule(ops)
    place = {i: k for k, i in enumerate(seq)}
    known, after, waits = {}, {}, {}
    for i in seq:
        o = ops[i]; kn = known.setdefault(o["e"], {}); mine = []
        for j in sorted(o["dep"], key=lambda j: -place[j]):
            key = ops[j]["sem"][0] if ops[j]["sem"] else ops[j]["e"]
            if kn.get(key, -1) >= place[j]: continue
            mine.append(j)
            for k, x in after[j].items():
                if kn.get(k, -1) < x: kn[k] = x
        waits[i] = mine
        after[i] = dict(kn); after[i][o["sem"][0] if o["sem"] else o["e"]] = place[i]
    need = set()
    for w in waits.values(): need.update(w)
    queue = {"V": g.vector, "S": g.scalar, "P": g.tensor, "G": g, "Y": g.sync}
    count, mark, waited = {}, {}, {}
    for i in seq:
        o = ops[i]; q = queue[o["e"]]
        for j in waits[i]:
            s, x = mark[j]
            q.wait_ge(T.sem[s], x); waited[s] = max(waited.get(s, 0), x)
        ins = o["fn"]()
        if o["sem"]:
            mark[i] = o["sem"]; count[o["sem"][0]] = o["sem"][1]
            if o["e"] != "G": ins.then_inc(T.sem[o["sem"][0]], 16)
        elif i in need:
            s = "c" + o["e"]; count[s] = count.get(s, 0) + 1; mark[i] = (s, count[s])
            ins.then_inc(T.sem[s], 1)
    g.wait_ge(T.sem.sent, total[0])
    for s, x in count.items():
        if waited.get(s, 0) < x: g.sync.wait_ge(T.sem[s], x)
